import numpy as np, ml_dtypes
CORES = [6,15,38,47]
N = 4
BF = ml_dtypes.bfloat16
def f(rng, *shape):
    return (rng.standard_normal(shape, dtype=np.float32) * np.exp2(rng.integers(-2, 3, shape[:-1] + (1,)))).astype(BF)
def wide(rng, *shape):
    v = f(rng, *shape).astype(np.float32); k = shape[:-2] + (1, shape[-1])
    return (v * np.exp2(rng.integers(-6, 7, k)) * (rng.random(k) > 0.0625)).astype(BF)
R, W, S, C = 32, 64, 3, 1
H = N * R
ROW, COL = np.arange(H)[None, :, None], np.arange(W)[None, None, :]
def stored(v):
    return np.ascontiguousarray(v.reshape(8, N, R, W).transpose(1, 0, 2, 3)).reshape(N, 8, R * W).astype(np.int32)
def whole(v):
    return np.ascontiguousarray(v.reshape(N, 8, R, W).transpose(1, 0, 2, 3)).reshape(8, H, W).astype(np.int64)
def field(rng):
    d = np.repeat(np.repeat(rng.integers(-1, 2, (2, 8, H // 8, W // 16)), 8, axis=2), 16, axis=3)
    d = np.roll(d, int(rng.integers(1, 8)), axis=2)
    return np.where(rng.random(d.shape) < 0.125, rng.integers(-1, 2, d.shape), d)
def inputs_of(rng, v):
    return {"vy": stored(v[0]), "vx": stored(v[1]), "img": f(rng, N, 128, C * R * W)}
def setup_inputs(rng):
    return inputs_of(rng, field(rng))
def setup_inputs_far(rng):
    v = np.zeros((2, 8, H, W), np.int64); o = rng.permutation(8)
    for k in range(8):
        v[0, o[k]] = 1 if k & 1 else -1; v[1, o[k]] = 1 if k & 2 else -1
        if k >= 4:
            m = rng.random((2, H, W)) < 0.015625
            v[:, o[k]] = np.where(m, rng.integers(-1, 2, (2, H, W)), v[:, o[k]])
    return inputs_of(rng, v)
def setup_inputs_ends(rng):
    v = field(rng); pm = np.array([-1, 1])
    for e in (0, H - 1): v[0, :, e, :] = rng.choice(pm, (8, W))
    for e in (0, W - 1): v[1, :, :, e] = rng.choice(pm, (8, H))
    v[0, :, 1, :] = np.where(rng.random((8, W)) < 0.75, -1, 1); v[0, :, H - 2, :] = np.where(rng.random((8, W)) < 0.75, 1, -1)
    v[1, :, :, 1] = np.where(rng.random((8, H)) < 0.75, -1, 1); v[1, :, :, W - 2] = np.where(rng.random((8, H)) < 0.75, 1, -1)
    o = rng.permutation(8); g, h = o[0], o[1]
    v[0, g, 0, :] = 2 * (np.arange(W) & 1) - 1; v[1, g, 0, :] = 1
    v[0, g, H - 1, :] = 2 * (np.arange(W) & 1) - 1; v[1, g, H - 1, :] = -1
    v[1, h, :, 0] = 2 * (np.arange(H) & 1) - 1; v[0, h, :, 0] = 1
    v[1, h, :, W - 1] = 2 * (np.arange(H) & 1) - 1; v[0, h, :, W - 1] = -1
    return inputs_of(rng, v)
def setup_inputs_sinks(rng):
    v = np.zeros((2, 8, H, W), np.int64); o = rng.permutation(8)
    v[1, o[1]] = 1 - 2 * (COL[0] & 1)
    v[0, o[2]] = 2 * (ROW[0] & 1) - 1
    for k in range(3, 8):
        r0, c0 = int(rng.integers(0, H)), int(rng.integers(0, W))
        if k == 3: r0 = R * int(rng.integers(1, N))
        if k == 4: r0 = R * int(rng.integers(1, N)) - 1
        v[0, o[k]] = np.sign(r0 - ROW[0]); v[1, o[k]] = np.sign(c0 - COL[0])
    return inputs_of(rng, v)
def setup_inputs_spread(rng):
    d = setup_inputs(rng); d["img"] = wide(rng, N, 128, C * R * W); return d
def check_inputs(d):
    bad = [k for k in ("vy", "vx") if not np.isin(np.asarray(d[k]), [-1, 0, 1]).all()]
    return bad + ([] if np.isfinite(np.asarray(d["img"]).astype(np.float32)).all() else ["finite"])
def place(a, b):
    return (ROW + a) % H, np.minimum(np.maximum(COL + b, 0), W - 1)
def reference(vy, vx, img):
    a, b = whole(vy), whole(vx); g = np.arange(8)[:, None, None]
    for s in range(S):
        p, q = place(a, b)
        a, b = a + a[g, p, q], b + b[g, p, q]
    p, q = place(a, b)
    u = np.ascontiguousarray(img.reshape(N, 8, 16, C, R, W).transpose(1, 0, 4, 5, 2, 3)).reshape(8, H, W, 16, C)
    z = u[g, p, q].reshape(8, N, R, W, 16, C)
    return {"y": np.ascontiguousarray(z.transpose(1, 0, 4, 5, 2, 3)).reshape(N, 128, C * R * W)}

@@ -1,0 +1,275 @@
+from concourse.bass import DstId, RemoteDMATransfer
+from concourse.mybir import AluOpType, ActivationFunctionType
+import comms_topo
+
+A = AluOpType
+AF = ActivationFunctionType
+B16, F32, I32, U16 = "bfloat16", "float32", "int32", "uint16"
+
+
+def bufs():
+    d = {}
+    for names, shape, ty in (
+            ("K1 b15 m16", [128, 1], I32), ("K4 t31", [128, 4], I32), ("U", [128, 144], F32), ("PI PC", [128, 16], F32),
+            ("PM PT", [128, 4, 2], F32), ("fc xf sc x0 t80 t64 w80 w64 hi", [128, 1], F32), ("tc", [128, 6], F32),
+            ("baseW", [128, 4, 64], F32), ("baseH", [128, 2, 64], F32), ("F S80 S64", [128, 144], B16),
+            ("SP SN", [128, 64], I32), ("WV", [128, 4, 64], I32), ("WB", [128, 4, 80], B16),
+            ("HL", [128, 2, 64], I32), ("HB", [128, 2, 80], B16), ("V0 V1 V2", [128, 3840], B16),
+            ("PHI", [128, 1152], B16), ("PHH", [128, 896], B16), ("L0I", [128, 150], U16), ("L1I", [128, 130], U16),
+            ("L0H L1H L3I", [128, 72], U16), ("L2IL L2IR", [128, 36], U16), ("L2HL L2HR", [128, 28], U16),
+            ("L3H", [128, 56], U16), ("IMG", [128, 3072], B16), ("Y", [128, 2048], B16)):
+        for nm in names.split():
+            d[nm] = ("sbuf", shape, ty)
+    for nm in "P0 P1 P2 P3 P4 P5 Q0".split():
+        d[nm] = ("psum", [128, 512], F32)
+    d["R0"] = ("psum", [128, 102, 5], F32)
+    return d
+
+
+SCRATCH = bufs()
+SEMAPHORES = ["st", "ow", "im", "imm", "hv", "hvl", "hm", "hml", "sto", "kc", "kg"] + ["e%d" % i for i in range(120)]
+
+
+def rank_program(g, core, T, topo):
+    rank = T.rank_of(core)
+    if rank is None:
+        return
+    n = len(T.cores)
+    prv, nxt = T.cores[(rank - 1) % n], T.cores[(rank + 1) % n]
+    V, S, P, Y = g.vector, g.scalar, g.tensor, g.sync
+    Q = {"v": V, "s": S, "p": P, "y": Y, "g": g}
+    sem = T.sem
+    total = {}
+    seen = {}
+
+    def ev(*calls):
+        nm = "e%d" % len(total)
+        total[nm] = len(calls)
+        for c in calls:
+            c.then_inc(sem[nm], 1)
+        return nm
+
+    def W(q, *evs):
+        for e in evs:
+            if (q, e) not in seen:
+                seen[(q, e)] = 1
+                Q[q].wait_ge(sem[e], total[e])
+
+    Y.dma_start(out=T.SP[0:64, :], in_=T.vx[:, 0:512]).then_inc(sem.st, 16)
+    S.dma_start(out=T.SP[64:128, :], in_=T.vy[:, 0:512]).then_inc(sem.st, 16)
+    Y.dma_start(out=T.SN[0:64, :], in_=T.vx[:, 1536:2048]).then_inc(sem.st, 16)
+    S.dma_start(out=T.SN[64:128, :], in_=T.vy[:, 1536:2048]).then_inc(sem.st, 16)
+    Y.dma_start(out=T.WV[0:64, :, :], in_=T.vx[:, :]).then_inc(sem.ow, 16)
+    S.dma_start(out=T.WV[64:128, :, :], in_=T.vy[:, :]).then_inc(sem.ow, 16)
+    Y.dma_start(out=T.IMG[:, 512:1024], in_=T.img[:, 0:512]).then_inc(sem.im, 16)
+    S.dma_start(out=T.IMG[:, 2048:2560], in_=T.img[:, 1536:2048]).then_inc(sem.im, 16)
+    Y.dma_start(out=T.IMG[:, 1024:2048], in_=T.img[:, 512:1536]).then_inc(sem.imm, 16)
+
+    for i in (g.iota(T.K1[:], [[0, 1]], 0, 1), g.iota(T.K4[:], [[1, 4]], 0, 4),
+              g.iota(T.U[:], [[1, 144]], 0, 0, allow_small_or_imprecise_dtypes=True),
+              g.iota(T.PM[:], [[0, 4], [2, 2]], -1, 0, allow_small_or_imprecise_dtypes=True),
+              g.iota(T.PI[:], [[9, 2], [1, 8]], -8, 0, allow_small_or_imprecise_dtypes=True)):
+        i.then_inc(sem.kg, 1)
+    kc = [0]
+
+    def K(ins):
+        ins.then_inc(sem.kc, 1)
+        kc[0] += 1
+
+    def KW():
+        V.wait_ge(sem.kc, kc[0])
+
+    ts = V.tensor_scalar
+    K(V.memset(T.tc[0:64, :], 0.0))
+    K(V.memset(T.WB[:], 0.0))
+    K(V.memset(T.HB[:], 0.0))
+    V.wait_ge(sem.kg, 5)
+    K(ts(T.t31[:], T.K4[:], 31, None, A.bitwise_and))
+    K(ts(T.b15[:], T.K1[:], 15, None, A.bitwise_and))
+    K(ts(T.m16[:], T.K1[:], 112, None, A.bitwise_and))
+    K(ts(T.fc[0:64, :], T.K1[0:64, :], 2.0, None, A.mult))
+    K(ts(T.fc[64:128, :], T.K1[64:128, :], 2.0, -127.0, A.mult, A.add))
+    K(ts(T.xf[:], T.K1[:], 64.0, None, A.is_lt))
+    KW()
+    K(ts(T.tc[64:128, 0:4], T.t31[64:128, :], 8.0, None, A.add))
+    K(ts(T.tc[64:128, 4:5], T.t31[64:128, 0:1], 0.25, None, A.mult))
+    K(ts(T.tc[64:128, 5:6], T.t31[64:128, 0:1], 0.25, 40.0, A.mult, A.add))
+    K(ts(T.sc[:], T.m16[:], 15.0, None, A.add))
+    K(ts(T.x0[:], T.b15[:], 0.0, None, A.is_equal))
+    K(ts(T.t80[:], T.b15[:], 1.0, 80.0, A.is_equal, A.mult))
+    K(ts(T.t64[:], T.b15[:], 1.0, 64.0, A.is_equal, A.mult))
+    K(ts(T.PT[:], T.PM[:], T.xf[:, 0:1], None, A.mult))
+    eF = ev(ts(T.F[:], T.U[:], T.fc[:, 0:1], None, A.is_equal))
+    KW()
+    for r in range(4):
+        K(ts(T.baseW[:, r, :], T.U[:, 0:64], T.xf[:, 0:1], T.tc[:, r:r + 1], A.mult, A.add))
+    K(V.tensor_tensor(T.w80[:], T.x0[:], T.t80[:], A.add))
+    K(V.tensor_tensor(T.w64[:], T.x0[:], T.t64[:], A.add))
+    KW()
+    eS80 = ev(ts(T.S80[:], T.U[:], T.sc[:, 0:1], T.w80[:, 0:1], A.is_equal, A.mult))
+    V.wait_ge(sem.ow, 32)
+    eWB = ev(V.tensor_tensor(T.WB[:, :, 8:72], T.WV[:], T.baseW[:], A.add))
+
+    es = {d: topo.engines(core, d) for d in (prv, nxt)}
+    h = min(len(es[prv]), len(es[nxt])) // 2
+
+    def send(src_p, dst_p, src_n, dst_n, rs, ls):
+        tr = []
+        for d, s, o, lo in ((prv, src_p, dst_p, 0), (nxt, src_n, dst_n, h)):
+            rid, pid, _ = topo.addr(d)
+            tr.append(RemoteDMATransfer(dst_ids=[DstId(rid=rid, pnc=pid)], dma_engine_mask=sum(1 << e for e in es[d][lo:lo + h]),
+                                        remote_sem=rs, src=s, dst=o))
+        g.remote_dma_fused(tr, local_sem=ls)
+
+    g.wait_ge(sem.st, 64)
+    send(T.SP[:], T.HL[:, 1, :], T.SN[:], T.HL[:, 0, :], sem.hv, sem.hvl)
+    g.wait_ge(sem.im, 32)
+    send(T.IMG[:, 512:1024], T.IMG[:, 2560:3072], T.IMG[:, 2048:2560], T.IMG[:, 0:512], sem.hm, sem.hml)
+
+    def pads(buf, i0, i1, w, *need):
+        W("s", ePC, *need)
+        W("v", ePC, *need)
+        v, a, z = T[buf], 80 * (i0 + 8), 80 * (i1 + 8)
+        c = []
+        for k in range(1, w + 1):
+            c.append(S.activation(v[:, a + 8 - k:z:80], v[:, a + 8:z:80], AF.Identity, bias=T.PC[:, 8 - k:9 - k]))
+            c.append(ts(v[:, a + 71 + k:z:80], v[:, a + 71:z:80], T.PC[:, 7 + k:8 + k], None, A.add))
+        return ev(*c)
+
+    def wrap(sel, parts, *need):
+        W("p", *need)
+        last = []
+        for out, src in parts:
+            for q in range(16):
+                ins = P.matmul(out, T[sel][:, 15 - q:143 - q], src(q), q == 0, q == 15)
+            last.append(ins)
+        return ev(*last)
+
+    def vp(buf, i0, i1, s=0):
+        return lambda q: T[buf][:, 80 * (i0 + 8) + s + q:80 * (i1 + 8) + s:16]
+
+    def lst(out, src, i0, i1, *need):
+        W("v", *need)
+        return ev(ts(out, src, float(8 - 80 * (i0 + 8)), float(80 * (i1 - i0) - 1), A.add, A.min))
+
+    def lst4(out, src, m, need):
+        W("v", need)
+        return ev(*[V.tensor_copy(out[:, 2 * f + b:4 * m:4], src[:, 2 * m * f + b:2 * m * (f + 1):2]) for f in (0, 1) for b in (0, 1)])
+
+    def gat(q, out, win, offs, need, clip=False):
+        W(q, *need)
+        if q == "s":
+            return ev(S.activation(out, win.indirect(offs), AF.Relu if clip else AF.Copy))
+        if clip:
+            return ev(ts(out, win.indirect(offs), T.hi[:, 0:1], None, A.min))
+        return ev(V.tensor_copy(out, win.indirect(offs)))
+
+    def rows(buf, i0, i1):
+        return T[buf][:, 80 * (i0 + 8):80 * (i1 + 8)]
+
+    W("v", eWB)
+    ePD = ev(V.tensor_tensor(T.WB[:, :, 7:73:65], T.WB[:, :, 8:72:63], T.PT[:], A.add))
+    W("p", eF, eWB, ePD)
+    eU = []
+    for b in range(6):
+        ms = range(3 * b, min(3 * b + 3, 16))
+        eU.append(ev(*[P.matmul(T["P%d" % b][:, 160 * k:160 * k + 160], T.F[:, 2 * (m // 2):2 * (m // 2) + 128],
+                                T.WB[:, 2 * (m % 2):2 * (m % 2) + 2, :], True, True) for k, m in enumerate(ms)]))
+    eC = []
+    for b in range(6):
+        i0, i1 = 6 * b, min(6 * b + 6, 32)
+        o, i = rows("V0", i0, i1), T["P%d" % b][:, 0:80 * (i1 - i0)]
+        W("sv"[b & 1], eU[b])
+        eC.append(ev(V.tensor_copy(o, i) if b & 1 else S.activation(o, i, AF.Copy)))
+    w0a = wrap("S80", [(T.Q0[:, 0:75], vp("V0", 1, 16))], eS80, *eC[0:3])
+    w0b = wrap("S80", [(T.P0[:, 0:75], vp("V0", 16, 31))], *eC)
+    K(ts(T.baseH[:, 0, :], T.U[:, 0:64], T.xf[:, 0:1], T.tc[:, 4:5], A.mult, A.add))
+    K(ts(T.baseH[:, 1, :], T.U[:, 0:64], T.xf[:, 0:1], T.tc[:, 5:6], A.mult, A.add))
+    ePC = ev(ts(T.PC[:], T.PI[:], T.x0[:, 0:1], None, A.mult))
+    eS64 = ev(ts(T.S64[:], T.U[:], T.sc[:, 0:1], T.w64[:, 0:1], A.is_equal, A.mult))
+    K(ts(T.hi[:], T.x0[:], 63.0 - 1024.0, 1024.0, A.mult, A.add))
+    l0a = lst(T.L0I[:, 0:75], T.Q0[:, 0:75], 0, 32, w0a)
+    l0b = lst(T.L0I[:, 75:150], T.P0[:, 0:75], 0, 32, w0b)
+    KW()
+
+    a0, a1, a3 = 16, 14, 10
+    need = [l0a, l0b] + eC
+    g0s = gat("s", rows("V1", 1, 1 + a0), rows("V0", 0, 32), T.L0I[:, 0:5 * a0], need)
+    g0v = gat("v", rows("V1", 1 + a0, 31), rows("V0", 0, 32), T.L0I[:, 5 * a0:150], need)
+    p1i = pads("V1", 1, 31, 2, g0s, g0v)
+
+    V.wait_ge(sem.hv, 2 * h)
+    eHB = ev(V.tensor_tensor(T.HB[:, :, 8:72], T.HL[:], T.baseH[:], A.add))
+    W("v", eHB)
+    eHD = ev(V.tensor_tensor(T.HB[:, :, 7:73:65], T.HB[:, :, 8:72:63], T.PT[:, 0:2, :], A.add))
+    W("p", eHB, eHD)
+
+    def unwrap(bank, part, ks):
+        return ev(*[P.matmul(T[bank][:, 80 * j:80 * j + 80], T.F[:, 2 * k:2 * k + 128], T.HB[:, part, :], True, True) for j, k in enumerate(ks)])
+    eUh = [unwrap("P1", 0, range(1, 5)), unwrap("P3", 1, range(0, 4)), unwrap("P2", 0, range(5, 8)), unwrap("P4", 1, range(4, 7))]
+    w1i = wrap("S80", [(T.P5[:, 0:130], vp("V1", 3, 29))], g0s, g0v, p1i)
+    eCh = []
+    for j, (b, q, i0, i1) in enumerate((("P1", "s", -7, -3), ("P3", "v", 32, 36), ("P2", "s", -3, 0), ("P4", "v", 36, 39))):
+        W(q, eUh[j])
+        o, i = rows("V0", i0, i1), T[b][:, 0:80 * (i1 - i0)]
+        eCh.append(ev(S.activation(o, i, AF.Copy) if q == "s" else V.tensor_copy(o, i)))
+    w0h = wrap("S80", [(T.Q0[:, 0:35], vp("V0", -6, 1)), (T.Q0[:, 35:70], vp("V0", 31, 38))], l0a, *eCh)
+
+    l1i = lst(T.L1I[:], T.P5[:, 0:130], 1, 31, w1i)
+    need = [g0s, g0v, p1i, l1i]
+    g1s = gat("s", rows("V2", 3, 3 + a1), rows("V1", 1, 31), T.L1I[:, 0:5 * a1], need)
+    g1v = gat("v", rows("V2", 3 + a1, 29), rows("V1", 1, 31), T.L1I[:, 5 * a1:130], need)
+    p2i = pads("V2", 3, 29, 4, g1s, g1v)
+
+    l0t = lst(T.L0H[:, 0:35], T.Q0[:, 0:35], -7, 2, w0h)
+    l0u = lst(T.L0H[:, 36:71], T.Q0[:, 35:70], 30, 39)
+    need = [l0t, l0u] + eCh
+    h0s = gat("s", rows("V1", -6, 1), rows("V0", -7, 2), T.L0H[:, 0:35], need)
+    h0v = gat("v", rows("V1", 31, 38), rows("V0", 30, 39), T.L0H[:, 36:71], need)
+    p1h = pads("V1", -6, 38, 2, h0s, h0v)
+
+    w2i = wrap("S80", [(T.R0[:, 0:18, :], vp("V2", 7, 25, 8))], g1s, g1v, p2i)
+    w1h = wrap("S80", [(T.P0[:, 0:35], vp("V1", -4, 3)), (T.P0[:, 35:70], vp("V1", 29, 36))], l0b, h0s, h0v, p1h)
+    l2l = lst(T.L2IL[:], T.R0[:, 0:18, 0:2], 3, 29, w2i)
+    l2r = lst(T.L2IR[:], T.R0[:, 0:18, 2:4], 3, 29)
+    need = [g1s, g1v, p2i, l2l, l2r]
+    g2s = gat("s", T.PHI[:, 0:576], rows("V2", 3, 29), T.L2IL[:], need, True)
+    g2v = gat("v", T.PHI[:, 576:1152], rows("V2", 3, 29), T.L2IR[:], need, True)
+
+    l1t = lst(T.L1H[:, 0:35], T.P0[:, 0:35], -6, 5, w1h)
+    l1u = lst(T.L1H[:, 36:71], T.P0[:, 35:70], 27, 38)
+    need = [l1t, l1u, h0s, h0v, g0s, g0v, p1h]
+    h1s = gat("s", rows("V2", -4, 3), rows("V1", -6, 5), T.L1H[:, 0:35], need)
+    h1v = gat("v", rows("V2", 29, 36), rows("V1", 27, 38), T.L1H[:, 36:71], need)
+    p2h = pads("V2", -4, 36, 4, h1s, h1v, g2s, g2v)
+
+    w3i = wrap("S64", [(T.P1[:, 0:72], lambda q: T.PHI[:, q:1152:16])], eS64, g2s, g2v)
+    w2h = wrap("S80", [(T.R0[:, 0:7, :], vp("V2", 0, 7, 8)), (T.R0[:, 7:14, :], vp("V2", 25, 32, 8))], l2l, l2r, h1s, h1v, p2h)
+    l3i = lst4(T.L3I, T.P1, 18, w3i)
+    for q in (V, S):
+        q.wait_ge(sem.im, 32)
+        q.wait_ge(sem.imm, 16)
+        q.wait_ge(sem.hm, 2 * h)
+    yi, ym, yj = 7 * 64, (7 + a3) * 64, 25 * 64
+    g3s = gat("s", T.Y[:, yi:ym], T.IMG[:], T.L3I[:, 0:4 * a3], [l3i])
+    g3v = gat("v", T.Y[:, ym:yj], T.IMG[:], T.L3I[:, 4 * a3:72], [l3i])
+    W("y", g3s, g3v)
+    Y.dma_start(out=T.y[:, yi:yj], in_=T.Y[:, yi:yj]).then_inc(sem.sto, 16)
+
+    l2hl = lst(T.L2HL[:], T.R0[:, 0:14, 0:2], -4, 36, w2h)
+    l2hr = lst(T.L2HR[:], T.R0[:, 0:14, 2:4], -4, 36)
+    need = [l2hl, l2hr, g1s, g1v, h1s, h1v, p2h]
+    h2s = gat("s", T.PHH[:, 0:448], rows("V2", -4, 36), T.L2HL[:], need, True)
+    h2v = gat("v", T.PHH[:, 448:896], rows("V2", -4, 36), T.L2HR[:], need, True)
+    w3h = wrap("S64", [(T.P2[:, 0:56], lambda q: T.PHH[:, q:896:16])], h2s, h2v)
+    l3h = lst4(T.L3H, T.P2, 14, w3h)
+    h3s = gat("s", T.Y[:, 0:yi], T.IMG[:], T.L3H[:, 0:28], [l3h])
+    h3v = gat("v", T.Y[:, yj:2048], T.IMG[:], T.L3H[:, 28:56], [l3h])
+    W("s", h3s)
+    S.dma_start(out=T.y[:, 0:yi], in_=T.Y[:, 0:yi]).then_inc(sem.sto, 16)
+    W("y", h3v)
+    Y.dma_start(out=T.y[:, yj:2048], in_=T.Y[:, yj:2048]).then_inc(sem.sto, 16)
+
+    Y.wait_ge(sem.sto, 48)
+    g.wait_ge(sem.hvl, 2 * h)
+    g.wait_ge(sem.hml, 2 * h)

@@ -11,23 +11,24 @@ def bufs():
     d = {}
     for names, shape, ty in (
             ("K1 b15 m16", [128, 1], I32), ("K4 t31", [128, 4], I32), ("U", [128, 144], F32), ("PI PC", [128, 16], F32),
-            ("PM PT", [128, 4, 2], F32), ("fc xf sc x0 t80 t64 w80 w64 hi", [128, 1], F32), ("tc", [128, 6], F32),
-            ("baseW", [128, 4, 64], F32), ("baseH", [128, 2, 64], F32), ("F S80 S64", [128, 144], B16),
-            ("SP SN", [128, 64], I32), ("WV", [128, 4, 64], I32), ("WB", [128, 4, 80], B16),
-            ("HL", [128, 2, 64], I32), ("HB", [128, 2, 80], B16), ("V0 V1 V2", [128, 3840], B16),
+            ("PM PT BW", [128, 4, 2], F32), ("BH", [128, 2, 2], F32), ("fc xf sc x0 t80 t64 w80 w64 hi", [128, 1], F32),
+            ("tc", [128, 6], F32), ("baseW", [128, 4, 64], F32), ("baseH", [128, 2, 64], F32),
+            ("F S80 S64", [128, 144], B16), ("ST", [128, 2, 64], I32), ("WV", [128, 4, 64], I32), ("WB", [128, 4, 80], B16),
+            ("HS HL", [128, 2, 80], B16), ("V0 V1 V2", [128, 3840], B16),
             ("PHI", [128, 1152], B16), ("PHH", [128, 896], B16), ("L0I", [128, 150], U16), ("L1I", [128, 130], U16),
             ("L0H L1H L3I", [128, 72], U16), ("L2IL L2IR", [128, 36], U16), ("L2HL L2HR", [128, 28], U16),
             ("L3H", [128, 56], U16), ("IMG", [128, 3072], B16), ("Y", [128, 2048], B16)):
         for nm in names.split():
             d[nm] = ("sbuf", shape, ty)
-    for nm in "P0 P1 P2 P3 P4 P5 Q0".split():
+    for nm in "P0 P1 P2 P3 P4 P5".split():
         d[nm] = ("psum", [128, 512], F32)
-    d["R0"] = ("psum", [128, 102, 5], F32)
+    for nm in "R0 R1".split():
+        d[nm] = ("psum", [128, 102, 5], F32)
     return d
 
 
 SCRATCH = bufs()
-SEMAPHORES = ["st", "ow", "im", "imm", "hv", "hvl", "hm", "hml", "sto", "kc", "kg"] + ["e%d" % i for i in range(120)]
+SEMAPHORES = ["st", "ow", "im", "imm", "hv", "hvl", "hm", "hml", "sto", "kc", "kg", "kh"] + ["e%d" % i for i in range(120)]
 
 
 def rank_program(g, core, T, topo):
@@ -55,21 +56,22 @@ def rank_program(g, core, T, topo):
                 seen[(q, e)] = 1
                 Q[q].wait_ge(sem[e], total[e])
 
-    Y.dma_start(out=T.SP[0:64, :], in_=T.vx[:, 0:512]).then_inc(sem.st, 16)
-    S.dma_start(out=T.SP[64:128, :], in_=T.vy[:, 0:512]).then_inc(sem.st, 16)
-    Y.dma_start(out=T.SN[0:64, :], in_=T.vx[:, 1536:2048]).then_inc(sem.st, 16)
-    S.dma_start(out=T.SN[64:128, :], in_=T.vy[:, 1536:2048]).then_inc(sem.st, 16)
+    Y.dma_start(out=T.ST[0:64, 1, :], in_=T.vx[:, 0:512]).then_inc(sem.st, 16)
+    S.dma_start(out=T.ST[64:128, 1, :], in_=T.vy[:, 0:512]).then_inc(sem.st, 16)
+    Y.dma_start(out=T.ST[0:64, 0, :], in_=T.vx[:, 1536:2048]).then_inc(sem.st, 16)
+    S.dma_start(out=T.ST[64:128, 0, :], in_=T.vy[:, 1536:2048]).then_inc(sem.st, 16)
     Y.dma_start(out=T.WV[0:64, :, :], in_=T.vx[:, :]).then_inc(sem.ow, 16)
     S.dma_start(out=T.WV[64:128, :, :], in_=T.vy[:, :]).then_inc(sem.ow, 16)
     Y.dma_start(out=T.IMG[:, 512:1024], in_=T.img[:, 0:512]).then_inc(sem.im, 16)
     S.dma_start(out=T.IMG[:, 2048:2560], in_=T.img[:, 1536:2048]).then_inc(sem.im, 16)
     Y.dma_start(out=T.IMG[:, 1024:2048], in_=T.img[:, 512:1536]).then_inc(sem.imm, 16)
 
-    for i in (g.iota(T.K1[:], [[0, 1]], 0, 1), g.iota(T.K4[:], [[1, 4]], 0, 4),
-              g.iota(T.U[:], [[1, 144]], 0, 0, allow_small_or_imprecise_dtypes=True),
+    for i in (g.iota(T.K4[:], [[1, 4]], 0, 4), g.iota(T.K1[:], [[0, 1]], 0, 1)):
+        i.then_inc(sem.kg, 1)
+    for i in (g.iota(T.U[:], [[1, 144]], 0, 0, allow_small_or_imprecise_dtypes=True),
               g.iota(T.PM[:], [[0, 4], [2, 2]], -1, 0, allow_small_or_imprecise_dtypes=True),
               g.iota(T.PI[:], [[9, 2], [1, 8]], -8, 0, allow_small_or_imprecise_dtypes=True)):
-        i.then_inc(sem.kg, 1)
+        i.then_inc(sem.kh, 1)
     kc = [0]
 
     def K(ins):
@@ -79,36 +81,47 @@ def rank_program(g, core, T, topo):
     def KW():
         V.wait_ge(sem.kc, kc[0])
 
-    ts = V.tensor_scalar
+    ts, tt = V.tensor_scalar, V.tensor_tensor
     K(V.memset(T.tc[0:64, :], 0.0))
+    K(V.memset(T.HS[:], 0.0))
     K(V.memset(T.WB[:], 0.0))
-    K(V.memset(T.HB[:], 0.0))
-    V.wait_ge(sem.kg, 5)
+    V.wait_ge(sem.kg, 2)
     K(ts(T.t31[:], T.K4[:], 31, None, A.bitwise_and))
+    K(ts(T.xf[:], T.K1[:], 64.0, None, A.is_lt))
     K(ts(T.b15[:], T.K1[:], 15, None, A.bitwise_and))
     K(ts(T.m16[:], T.K1[:], 112, None, A.bitwise_and))
     K(ts(T.fc[0:64, :], T.K1[0:64, :], 2.0, None, A.mult))
     K(ts(T.fc[64:128, :], T.K1[64:128, :], 2.0, -127.0, A.mult, A.add))
-    K(ts(T.xf[:], T.K1[:], 64.0, None, A.is_lt))
     KW()
-    K(ts(T.tc[64:128, 0:4], T.t31[64:128, :], 8.0, None, A.add))
     K(ts(T.tc[64:128, 4:5], T.t31[64:128, 0:1], 0.25, None, A.mult))
     K(ts(T.tc[64:128, 5:6], T.t31[64:128, 0:1], 0.25, 40.0, A.mult, A.add))
+    K(ts(T.tc[64:128, 0:4], T.t31[64:128, :], 8.0, None, A.add))
     K(ts(T.sc[:], T.m16[:], 15.0, None, A.add))
     K(ts(T.x0[:], T.b15[:], 0.0, None, A.is_equal))
     K(ts(T.t80[:], T.b15[:], 1.0, 80.0, A.is_equal, A.mult))
-    K(ts(T.t64[:], T.b15[:], 1.0, 64.0, A.is_equal, A.mult))
+    V.wait_ge(sem.kh, 3)
     K(ts(T.PT[:], T.PM[:], T.xf[:, 0:1], None, A.mult))
     eF = ev(ts(T.F[:], T.U[:], T.fc[:, 0:1], None, A.is_equal))
     KW()
+    K(tt(T.w80[:], T.x0[:], T.t80[:], A.add))
+    for p in (0, 1):
+        K(ts(T.baseH[:, p, :], T.U[:, 0:64], T.xf[:, 0:1], T.tc[:, 4 + p:5 + p], A.mult, A.add))
     for r in range(4):
         K(ts(T.baseW[:, r, :], T.U[:, 0:64], T.xf[:, 0:1], T.tc[:, r:r + 1], A.mult, A.add))
-    K(V.tensor_tensor(T.w80[:], T.x0[:], T.t80[:], A.add))
-    K(V.tensor_tensor(T.w64[:], T.x0[:], T.t64[:], A.add))
     KW()
-    eS80 = ev(ts(T.S80[:], T.U[:], T.sc[:, 0:1], T.w80[:, 0:1], A.is_equal, A.mult))
+    K(tt(T.BH[:], T.baseH[:, :, 0:64:63], T.PT[:, 0:2, :], A.add))
+    K(tt(T.BW[:], T.baseW[:, :, 0:64:63], T.PT[:], A.add))
+    KW()
+    V.wait_ge(sem.st, 64)
+    eHS = ev(tt(T.HS[:, :, 8:72], T.ST[:], T.baseH[:], A.add))
+    eHD = ev(tt(T.HS[:, :, 7:73:65], T.ST[:, :, 0:64:63], T.BH[:], A.add))
+    eBW = ev(V.tensor_copy(T.P5[:, 0:256], T.baseW[:]))
+    W("v", eBW)
     V.wait_ge(sem.ow, 32)
-    eWB = ev(V.tensor_tensor(T.WB[:, :, 8:72], T.WV[:], T.baseW[:], A.add))
+    eWB = ev(tt(T.WB[:, :, 8:72], T.WV[:], T.P5[:, 0:256], A.add))
+    ePD = ev(tt(T.WB[:, :, 7:73:65], T.WV[:, :, 0:64:63], T.BW[:], A.add))
+    eS80 = ev(ts(T.S80[:], T.U[:], T.sc[:, 0:1], T.w80[:, 0:1], A.is_equal, A.mult))
+    K(ts(T.t64[:], T.b15[:], 1.0, 64.0, A.is_equal, A.mult))
 
     es = {d: topo.engines(core, d) for d in (prv, nxt)}
     h = min(len(es[prv]), len(es[nxt])) // 2
@@ -121,8 +134,8 @@ def rank_program(g, core, T, topo):
                                         remote_sem=rs, src=s, dst=o))
         g.remote_dma_fused(tr, local_sem=ls)
 
-    g.wait_ge(sem.st, 64)
-    send(T.SP[:], T.HL[:, 1, :], T.SN[:], T.HL[:, 0, :], sem.hv, sem.hvl)
+    W("g", eHS, eHD)
+    send(T.HS[:, 1, :], T.HL[:, 1, :], T.HS[:, 0, :], T.HL[:, 0, :], sem.hv, sem.hvl)
     g.wait_ge(sem.im, 32)
     send(T.IMG[:, 512:1024], T.IMG[:, 2560:3072], T.IMG[:, 2048:2560], T.IMG[:, 0:512], sem.hm, sem.hml)
 
@@ -167,8 +180,6 @@ def rank_program(g, core, T, topo):
     def rows(buf, i0, i1):
         return T[buf][:, 80 * (i0 + 8):80 * (i1 + 8)]
 
-    W("v", eWB)
-    ePD = ev(V.tensor_tensor(T.WB[:, :, 7:73:65], T.WB[:, :, 8:72:63], T.PT[:], A.add))
     W("p", eF, eWB, ePD)
     eU = []
     for b in range(6):
@@ -181,87 +192,87 @@ def rank_program(g, core, T, topo):
         o, i = rows("V0", i0, i1), T["P%d" % b][:, 0:80 * (i1 - i0)]
         W("sv"[b & 1], eU[b])
         eC.append(ev(V.tensor_copy(o, i) if b & 1 else S.activation(o, i, AF.Copy)))
-    w0a = wrap("S80", [(T.Q0[:, 0:75], vp("V0", 1, 16))], eS80, *eC[0:3])
-    w0b = wrap("S80", [(T.P0[:, 0:75], vp("V0", 16, 31))], *eC)
-    K(ts(T.baseH[:, 0, :], T.U[:, 0:64], T.xf[:, 0:1], T.tc[:, 4:5], A.mult, A.add))
-    K(ts(T.baseH[:, 1, :], T.U[:, 0:64], T.xf[:, 0:1], T.tc[:, 5:6], A.mult, A.add))
-    ePC = ev(ts(T.PC[:], T.PI[:], T.x0[:, 0:1], None, A.mult))
-    eS64 = ev(ts(T.S64[:], T.U[:], T.sc[:, 0:1], T.w64[:, 0:1], A.is_equal, A.mult))
-    K(ts(T.hi[:], T.x0[:], 63.0 - 1024.0, 1024.0, A.mult, A.add))
-    l0a = lst(T.L0I[:, 0:75], T.Q0[:, 0:75], 0, 32, w0a)
-    l0b = lst(T.L0I[:, 75:150], T.P0[:, 0:75], 0, 32, w0b)
+    w0a = wrap("S80", [(T.R0[:, 0:16, :], vp("V0", 1, 17))], eS80, *eC[0:3])
+    w0b = wrap("S80", [(T.R1[:, 0:14, :], vp("V0", 17, 31))], *eC)
     KW()
+    K(tt(T.w64[:], T.x0[:], T.t64[:], A.add))
+    ePC = ev(ts(T.PC[:], T.PI[:], T.x0[:, 0:1], None, A.mult))
+    K(ts(T.hi[:], T.x0[:], 63.0 - 1024.0, 1024.0, A.mult, A.add))
+    KW()
+    eS64 = ev(ts(T.S64[:], T.U[:], T.sc[:, 0:1], T.w64[:, 0:1], A.is_equal, A.mult))
 
-    a0, a1, a3 = 16, 14, 10
-    need = [l0a, l0b] + eC
-    g0s = gat("s", rows("V1", 1, 1 + a0), rows("V0", 0, 32), T.L0I[:, 0:5 * a0], need)
-    g0v = gat("v", rows("V1", 1 + a0, 31), rows("V0", 0, 32), T.L0I[:, 5 * a0:150], need)
-    p1i = pads("V1", 1, 31, 2, g0s, g0v)
-
-    V.wait_ge(sem.hv, 2 * h)
-    eHB = ev(V.tensor_tensor(T.HB[:, :, 8:72], T.HL[:], T.baseH[:], A.add))
-    W("v", eHB)
-    eHD = ev(V.tensor_tensor(T.HB[:, :, 7:73:65], T.HB[:, :, 8:72:63], T.PT[:, 0:2, :], A.add))
-    W("p", eHB, eHD)
+    l0a = lst(T.L0I[:, 0:80], T.R0[:, 0:16, :], 0, 18, w0a)
+    need = [l0a] + eC[0:3]
+    gas = gat("s", rows("V1", 1, 9), rows("V0", 0, 18), T.L0I[:, 0:40], need)
+    gav = gat("v", rows("V1", 9, 17), rows("V0", 0, 18), T.L0I[:, 40:80], need)
+    w1a = wrap("S80", [(T.P0[:, 0:60], vp("V1", 3, 15))], gas, gav)
+    l0b = lst(T.L0I[:, 80:150], T.R1[:, 0:14, :], 16, 32, w0b)
+    need = [l0b] + eC
+    gbs = gat("s", rows("V1", 17, 25), rows("V0", 16, 32), T.L0I[:, 80:120], need)
+    gbv = gat("v", rows("V1", 25, 31), rows("V0", 16, 32), T.L0I[:, 120:150], need)
+    p1i = pads("V1", 1, 31, 2, gas, gav, gbs, gbv, w1a)
 
     def unwrap(bank, part, ks):
-        return ev(*[P.matmul(T[bank][:, 80 * j:80 * j + 80], T.F[:, 2 * k:2 * k + 128], T.HB[:, part, :], True, True) for j, k in enumerate(ks)])
+        return ev(*[P.matmul(T[bank][:, 80 * j:80 * j + 80], T.F[:, 2 * k:2 * k + 128], T.HL[:, part, :], True, True) for j, k in enumerate(ks)])
+    P.wait_ge(sem.hv, 2 * h)
     eUh = [unwrap("P1", 0, range(1, 5)), unwrap("P3", 1, range(0, 4)), unwrap("P2", 0, range(5, 8)), unwrap("P4", 1, range(4, 7))]
-    w1i = wrap("S80", [(T.P5[:, 0:130], vp("V1", 3, 29))], g0s, g0v, p1i)
     eCh = []
     for j, (b, q, i0, i1) in enumerate((("P1", "s", -7, -3), ("P3", "v", 32, 36), ("P2", "s", -3, 0), ("P4", "v", 36, 39))):
         W(q, eUh[j])
         o, i = rows("V0", i0, i1), T[b][:, 0:80 * (i1 - i0)]
         eCh.append(ev(S.activation(o, i, AF.Copy) if q == "s" else V.tensor_copy(o, i)))
-    w0h = wrap("S80", [(T.Q0[:, 0:35], vp("V0", -6, 1)), (T.Q0[:, 35:70], vp("V0", 31, 38))], l0a, *eCh)
+    w0h = wrap("S80", [(T.R0[:, 0:7, :], vp("V0", -6, 1)), (T.R0[:, 7:14, :], vp("V0", 31, 38))], l0a, *eCh)
+    w1b = wrap("S80", [(T.P5[:, 0:70], vp("V1", 15, 29))], p1i)
 
-    l1i = lst(T.L1I[:], T.P5[:, 0:130], 1, 31, w1i)
-    need = [g0s, g0v, p1i, l1i]
-    g1s = gat("s", rows("V2", 3, 3 + a1), rows("V1", 1, 31), T.L1I[:, 0:5 * a1], need)
-    g1v = gat("v", rows("V2", 3 + a1, 29), rows("V1", 1, 31), T.L1I[:, 5 * a1:130], need)
-    p2i = pads("V2", 3, 29, 4, g1s, g1v)
+    l1a = lst(T.L1I[:, 0:60], T.P0[:, 0:60], 1, 17, w1a)
+    need = [gas, gav, p1i, l1a]
+    g1s = gat("s", rows("V2", 3, 9), rows("V1", 1, 17), T.L1I[:, 0:30], need)
+    g1v = gat("v", rows("V2", 9, 15), rows("V1", 1, 17), T.L1I[:, 30:60], need)
 
-    l0t = lst(T.L0H[:, 0:35], T.Q0[:, 0:35], -7, 2, w0h)
-    l0u = lst(T.L0H[:, 36:71], T.Q0[:, 35:70], 30, 39)
+    l0t = lst(T.L0H[:, 0:35], T.R0[:, 0:7, :], -7, 2, w0h)
+    l0u = lst(T.L0H[:, 36:71], T.R0[:, 7:14, :], 30, 39)
     need = [l0t, l0u] + eCh
     h0s = gat("s", rows("V1", -6, 1), rows("V0", -7, 2), T.L0H[:, 0:35], need)
     h0v = gat("v", rows("V1", 31, 38), rows("V0", 30, 39), T.L0H[:, 36:71], need)
-    p1h = pads("V1", -6, 38, 2, h0s, h0v)
+    l1b = lst(T.L1I[:, 60:130], T.P5[:, 0:70], 13, 31, w1b)
+    p1h = pads("V1", -6, 38, 2, h0s, h0v, w1b, g1s, g1v)
+    w1h = wrap("S80", [(T.P0[:, 0:35], vp("V1", -4, 3)), (T.P0[:, 35:70], vp("V1", 29, 36))], l1a, h0s, h0v, p1h)
 
-    w2i = wrap("S80", [(T.R0[:, 0:18, :], vp("V2", 7, 25, 8))], g1s, g1v, p2i)
-    w1h = wrap("S80", [(T.P0[:, 0:35], vp("V1", -4, 3)), (T.P0[:, 35:70], vp("V1", 29, 36))], l0b, h0s, h0v, p1h)
-    l2l = lst(T.L2IL[:], T.R0[:, 0:18, 0:2], 3, 29, w2i)
-    l2r = lst(T.L2IR[:], T.R0[:, 0:18, 2:4], 3, 29)
-    need = [g1s, g1v, p2i, l2l, l2r]
-    g2s = gat("s", T.PHI[:, 0:576], rows("V2", 3, 29), T.L2IL[:], need, True)
-    g2v = gat("v", T.PHI[:, 576:1152], rows("V2", 3, 29), T.L2IR[:], need, True)
-
+    need = [gas, gav, gbs, gbv, p1h, l1b]
+    g2s = gat("s", rows("V2", 15, 23), rows("V1", 13, 31), T.L1I[:, 60:100], need)
+    g2v = gat("v", rows("V2", 23, 29), rows("V1", 13, 31), T.L1I[:, 100:130], need)
+    w2i = wrap("S80", [(T.R1[:, 0:18, :], vp("V2", 7, 25, 8))], l0b, g1s, g1v, g2s, g2v)
     l1t = lst(T.L1H[:, 0:35], T.P0[:, 0:35], -6, 5, w1h)
     l1u = lst(T.L1H[:, 36:71], T.P0[:, 35:70], 27, 38)
-    need = [l1t, l1u, h0s, h0v, g0s, g0v, p1h]
+    need = [l1t, l1u, h0s, h0v, gas, gav, gbs, gbv, p1h]
     h1s = gat("s", rows("V2", -4, 3), rows("V1", -6, 5), T.L1H[:, 0:35], need)
     h1v = gat("v", rows("V2", 29, 36), rows("V1", 27, 38), T.L1H[:, 36:71], need)
-    p2h = pads("V2", -4, 36, 4, h1s, h1v, g2s, g2v)
+    p2 = pads("V2", -4, 36, 4, h1s, h1v, g1s, g1v, g2s, g2v, w2i)
+    w2h = wrap("S80", [(T.R0[:, 0:7, :], vp("V2", 0, 7, 8)), (T.R0[:, 7:14, :], vp("V2", 25, 32, 8))], l0t, l0u, h1s, h1v, p2)
 
-    w3i = wrap("S64", [(T.P1[:, 0:72], lambda q: T.PHI[:, q:1152:16])], eS64, g2s, g2v)
-    w2h = wrap("S80", [(T.R0[:, 0:7, :], vp("V2", 0, 7, 8)), (T.R0[:, 7:14, :], vp("V2", 25, 32, 8))], l2l, l2r, h1s, h1v, p2h)
+    all2 = [h1s, h1v, g1s, g1v, g2s, g2v, p2]
+    l2l = lst(T.L2IL[:], T.R1[:, 0:18, 0:2], 3, 29, w2i)
+    l2r = lst(T.L2IR[:], T.R1[:, 0:18, 2:4], 3, 29)
+    i2s = gat("s", T.PHI[:, 0:576], rows("V2", 3, 29), T.L2IL[:], [l2l, l2r] + all2, True)
+    i2v = gat("v", T.PHI[:, 576:1152], rows("V2", 3, 29), T.L2IR[:], [l2l, l2r] + all2, True)
+    w3i = wrap("S64", [(T.P1[:, 0:72], lambda q: T.PHI[:, q:1152:16])], eS64, i2s, i2v)
+    l2hl = lst(T.L2HL[:], T.R0[:, 0:14, 0:2], -4, 36, w2h)
+    l2hr = lst(T.L2HR[:], T.R0[:, 0:14, 2:4], -4, 36)
+    h2s = gat("s", T.PHH[:, 0:448], rows("V2", -4, 36), T.L2HL[:], [l2hl, l2hr] + all2, True)
+    h2v = gat("v", T.PHH[:, 448:896], rows("V2", -4, 36), T.L2HR[:], [l2hl, l2hr] + all2, True)
+    w3h = wrap("S64", [(T.P2[:, 0:56], lambda q: T.PHH[:, q:896:16])], h2s, h2v)
+
     l3i = lst4(T.L3I, T.P1, 18, w3i)
     for q in (V, S):
         q.wait_ge(sem.im, 32)
         q.wait_ge(sem.imm, 16)
         q.wait_ge(sem.hm, 2 * h)
+    a3 = 10
     yi, ym, yj = 7 * 64, (7 + a3) * 64, 25 * 64
     g3s = gat("s", T.Y[:, yi:ym], T.IMG[:], T.L3I[:, 0:4 * a3], [l3i])
     g3v = gat("v", T.Y[:, ym:yj], T.IMG[:], T.L3I[:, 4 * a3:72], [l3i])
     W("y", g3s, g3v)
     Y.dma_start(out=T.y[:, yi:yj], in_=T.Y[:, yi:yj]).then_inc(sem.sto, 16)
-
-    l2hl = lst(T.L2HL[:], T.R0[:, 0:14, 0:2], -4, 36, w2h)
-    l2hr = lst(T.L2HR[:], T.R0[:, 0:14, 2:4], -4, 36)
-    need = [l2hl, l2hr, g1s, g1v, h1s, h1v, p2h]
-    h2s = gat("s", T.PHH[:, 0:448], rows("V2", -4, 36), T.L2HL[:], need, True)
-    h2v = gat("v", T.PHH[:, 448:896], rows("V2", -4, 36), T.L2HR[:], need, True)
-    w3h = wrap("S64", [(T.P2[:, 0:56], lambda q: T.PHH[:, q:896:16])], h2s, h2v)
     l3h = lst4(T.L3H, T.P2, 14, w3h)
     h3s = gat("s", T.Y[:, 0:yi], T.IMG[:], T.L3H[:, 0:28], [l3h])
     h3v = gat("v", T.Y[:, yj:2048], T.IMG[:], T.L3H[:, 28:56], [l3h])

@@ -5,19 +5,20 @@ import comms_topo
 A = AluOpType
 AF = ActivationFunctionType
 B16, F32, I32, U16 = "bfloat16", "float32", "int32", "uint16"
+IO = 6
+M = 32 - 2 * IO
 
 
 def bufs():
     d = {}
     for names, shape, ty in (
-            ("K1 b15 m16", [128, 1], I32), ("K4 t31", [128, 4], I32), ("U", [128, 144], F32), ("PI PC", [128, 16], F32),
-            ("PM PT BW", [128, 4, 2], F32), ("BH", [128, 2, 2], F32), ("fc xf sc x0 t80 t64 w80 w64 hi", [128, 1], F32),
-            ("tc", [128, 6], F32), ("baseW", [128, 4, 64], F32), ("baseH", [128, 2, 64], F32),
-            ("F S80 S64", [128, 144], B16), ("ST", [128, 2, 64], I32), ("WV", [128, 4, 64], I32), ("WB", [128, 4, 80], B16),
-            ("HS HL", [128, 2, 80], B16), ("V0 V1 V2", [128, 3840], B16),
-            ("PHI", [128, 1152], B16), ("PHH", [128, 896], B16), ("L0I", [128, 150], U16), ("L1I", [128, 130], U16),
-            ("L0H L1H L3I", [128, 72], U16), ("L2IL L2IR", [128, 36], U16), ("L2HL L2HR", [128, 28], U16),
-            ("L3H", [128, 56], U16), ("IMG", [128, 3072], B16), ("Y", [128, 2048], B16)):
+            ("b15 m16", [128, 1], I32), ("K4 t7 RR", [128, 4], I32), ("U", [128, 144], F32), ("PI PC", [128, 16], F32),
+            ("BW", [128, 4, 2], F32), ("fc xf sc x0 tp tm t80 t64 w80 w64 hi", [128, 1], F32), ("tc", [128, 4], F32),
+            ("F S80 S64", [128, 144], B16), ("WV", [128, 4, 64], I32), ("WB", [128, 4, 80], B16),
+            ("HL", [128, 2, 80], B16), ("V0 V1 V2", [128, 3840], B16),
+            ("PHI", [128, 64 * M], B16), ("PHH", [128, 128 * IO], B16), ("L0I", [128, 150], U16), ("L1I", [128, 140], U16),
+            ("L0H L1H", [128, 72], U16), ("L2IL L2IR", [128, 2 * M], U16), ("L2HL", [128, 6 * IO], U16), ("L2HR", [128, 2 * IO], U16),
+            ("L3I", [128, 4 * M], U16), ("L3H", [128, 8 * IO], U16), ("IMG", [128, 3072], B16), ("Y", [128, 2048], B16)):
         for nm in names.split():
             d[nm] = ("sbuf", shape, ty)
     for nm in "P0 P1 P2 P3 P4 P5".split():
@@ -28,7 +29,7 @@ def bufs():
 
 
 SCRATCH = bufs()
-SEMAPHORES = ["st", "ow", "im", "imm", "hv", "hvl", "hm", "hml", "sto", "kc", "kg", "kh"] + ["e%d" % i for i in range(120)]
+SEMAPHORES = ["oa", "ow", "im", "imm", "hv", "hvl", "hm", "hml", "sto", "kc", "kg", "kh", "kp"] + ["e%d" % i for i in range(120)]
 
 
 def rank_program(g, core, T, topo):
@@ -56,22 +57,18 @@ def rank_program(g, core, T, topo):
                 seen[(q, e)] = 1
                 Q[q].wait_ge(sem[e], total[e])
 
-    Y.dma_start(out=T.ST[0:64, 1, :], in_=T.vx[:, 0:512]).then_inc(sem.st, 16)
-    S.dma_start(out=T.ST[64:128, 1, :], in_=T.vy[:, 0:512]).then_inc(sem.st, 16)
-    Y.dma_start(out=T.ST[0:64, 0, :], in_=T.vx[:, 1536:2048]).then_inc(sem.st, 16)
-    S.dma_start(out=T.ST[64:128, 0, :], in_=T.vy[:, 1536:2048]).then_inc(sem.st, 16)
-    Y.dma_start(out=T.WV[0:64, :, :], in_=T.vx[:, :]).then_inc(sem.ow, 16)
-    S.dma_start(out=T.WV[64:128, :, :], in_=T.vy[:, :]).then_inc(sem.ow, 16)
+    SLOT = (0, 2, 3, 1)
+    for r in (0, 3, 1, 2):
+        sm = sem.oa if r in (0, 3) else sem.ow
+        Y.dma_start(out=T.WV[0:64, SLOT[r], :], in_=T.vx[:, 512 * r:512 * r + 512]).then_inc(sm, 16)
+        S.dma_start(out=T.WV[64:128, SLOT[r], :], in_=T.vy[:, 512 * r:512 * r + 512]).then_inc(sm, 16)
     Y.dma_start(out=T.IMG[:, 512:1024], in_=T.img[:, 0:512]).then_inc(sem.im, 16)
     S.dma_start(out=T.IMG[:, 2048:2560], in_=T.img[:, 1536:2048]).then_inc(sem.im, 16)
     Y.dma_start(out=T.IMG[:, 1024:2048], in_=T.img[:, 512:1536]).then_inc(sem.imm, 16)
 
-    for i in (g.iota(T.K4[:], [[1, 4]], 0, 4), g.iota(T.K1[:], [[0, 1]], 0, 1)):
-        i.then_inc(sem.kg, 1)
-    for i in (g.iota(T.U[:], [[1, 144]], 0, 0, allow_small_or_imprecise_dtypes=True),
-              g.iota(T.PM[:], [[0, 4], [2, 2]], -1, 0, allow_small_or_imprecise_dtypes=True),
-              g.iota(T.PI[:], [[9, 2], [1, 8]], -8, 0, allow_small_or_imprecise_dtypes=True)):
-        i.then_inc(sem.kh, 1)
+    for o, pat, b0, cm, sm in ((T.K4, [[0, 4]], 0, 1, sem.kg), (T.RR, [[8, 4]], 8, 0, sem.kg), (T.U, [[1, 144]], 0, 0, sem.kh),
+                               (T.PI, [[9, 2], [1, 8]], -8, 0, sem.kp)):
+        g.iota(o[:], pat, b0, cm, allow_small_or_imprecise_dtypes=True).then_inc(sm, 1)
     kc = [0]
 
     def K(ins):
@@ -82,46 +79,40 @@ def rank_program(g, core, T, topo):
         V.wait_ge(sem.kc, kc[0])
 
     ts, tt = V.tensor_scalar, V.tensor_tensor
-    K(V.memset(T.tc[0:64, :], 0.0))
-    K(V.memset(T.HS[:], 0.0))
+    e0 = ev(V.memset(T.tc[0:64, :], 0.0))
     K(V.memset(T.WB[:], 0.0))
     V.wait_ge(sem.kg, 2)
-    K(ts(T.t31[:], T.K4[:], 31, None, A.bitwise_and))
-    K(ts(T.xf[:], T.K1[:], 64.0, None, A.is_lt))
-    K(ts(T.b15[:], T.K1[:], 15, None, A.bitwise_and))
-    K(ts(T.m16[:], T.K1[:], 112, None, A.bitwise_and))
-    K(ts(T.fc[0:64, :], T.K1[0:64, :], 2.0, None, A.mult))
-    K(ts(T.fc[64:128, :], T.K1[64:128, :], 2.0, -127.0, A.mult, A.add))
+    K(ts(T.t7[:], T.K4[:], 7, None, A.bitwise_and))
+    exf = ev(ts(T.xf[:], T.K4[:, 0:1], 64.0, None, A.is_lt))
+    K(ts(T.fc[0:64, :], T.K4[0:64, 0:1], 2.0, None, A.mult))
+    K(ts(T.fc[64:128, :], T.K4[64:128, 0:1], 2.0, -127.0, A.mult, A.add))
     KW()
-    K(ts(T.tc[64:128, 4:5], T.t31[64:128, 0:1], 0.25, None, A.mult))
-    K(ts(T.tc[64:128, 5:6], T.t31[64:128, 0:1], 0.25, 40.0, A.mult, A.add))
-    K(ts(T.tc[64:128, 0:4], T.t31[64:128, :], 8.0, None, A.add))
-    K(ts(T.sc[:], T.m16[:], 15.0, None, A.add))
+    etc = ev(tt(T.tc[64:128, :], T.t7[64:128, :], T.RR[64:128, :], A.add))
+    V.wait_ge(sem.kh, 1)
+    eF = ev(ts(T.F[:], T.U[:], T.fc[:, 0:1], None, A.is_equal))
+    S.wait_ge(sem.kh, 1)
+    W("s", e0, exf, etc)
+    ebw = ev(*[S.activation(T.P5[:, 64 * SLOT[r]:64 * SLOT[r] + 64], T.U[:, 0:64], AF.Identity, bias=T.tc[:, r:r + 1], scale=T.xf[:, 0:1]) for r in range(4)])
+    W("v", exf, ebw)
+    K(ts(T.BW[:, :, 0], T.P5[:, 0:256:64], T.xf[:, 0:1], None, A.subtract))
+    K(ts(T.BW[:, :, 1], T.P5[:, 63:256:64], T.xf[:, 0:1], None, A.add))
+    KW()
+    eWB = []
+    for sm, a in ((sem.oa, 0), (sem.ow, 2)):
+        V.wait_ge(sm, 64)
+        eWB.append(ev(tt(T.WB[:, a:a + 2, 8:72], T.WV[:, a:a + 2, :], T.P5[:, 64 * a:64 * a + 128], A.add),
+                      tt(T.WB[:, a:a + 2, 7:73:65], T.WV[:, a:a + 2, 0:64:63], T.BW[:, a:a + 2, :], A.add)))
+    K(ts(T.b15[:], T.K4[:, 0:1], 15, None, A.bitwise_and))
+    K(ts(T.m16[:], T.K4[:, 0:1], 112, None, A.bitwise_and))
+    KW()
     K(ts(T.x0[:], T.b15[:], 0.0, None, A.is_equal))
     K(ts(T.t80[:], T.b15[:], 1.0, 80.0, A.is_equal, A.mult))
-    V.wait_ge(sem.kh, 3)
-    K(ts(T.PT[:], T.PM[:], T.xf[:, 0:1], None, A.mult))
-    eF = ev(ts(T.F[:], T.U[:], T.fc[:, 0:1], None, A.is_equal))
+    K(ts(T.sc[:], T.m16[:], 15.0, None, A.add))
     KW()
     K(tt(T.w80[:], T.x0[:], T.t80[:], A.add))
-    for p in (0, 1):
-        K(ts(T.baseH[:, p, :], T.U[:, 0:64], T.xf[:, 0:1], T.tc[:, 4 + p:5 + p], A.mult, A.add))
-    for r in range(4):
-        K(ts(T.baseW[:, r, :], T.U[:, 0:64], T.xf[:, 0:1], T.tc[:, r:r + 1], A.mult, A.add))
-    KW()
-    K(tt(T.BH[:], T.baseH[:, :, 0:64:63], T.PT[:, 0:2, :], A.add))
-    K(tt(T.BW[:], T.baseW[:, :, 0:64:63], T.PT[:], A.add))
-    KW()
-    V.wait_ge(sem.st, 64)
-    eHS = ev(tt(T.HS[:, :, 8:72], T.ST[:], T.baseH[:], A.add))
-    eHD = ev(tt(T.HS[:, :, 7:73:65], T.ST[:, :, 0:64:63], T.BH[:], A.add))
-    eBW = ev(V.tensor_copy(T.P5[:, 0:256], T.baseW[:]))
-    W("v", eBW)
-    V.wait_ge(sem.ow, 32)
-    eWB = ev(tt(T.WB[:, :, 8:72], T.WV[:], T.P5[:, 0:256], A.add))
-    ePD = ev(tt(T.WB[:, :, 7:73:65], T.WV[:, :, 0:64:63], T.BW[:], A.add))
-    eS80 = ev(ts(T.S80[:], T.U[:], T.sc[:, 0:1], T.w80[:, 0:1], A.is_equal, A.mult))
     K(ts(T.t64[:], T.b15[:], 1.0, 64.0, A.is_equal, A.mult))
+    KW()
+    eS80 = ev(ts(T.S80[:], T.U[:], T.sc[:, 0:1], T.w80[:, 0:1], A.is_equal, A.mult))
 
     es = {d: topo.engines(core, d) for d in (prv, nxt)}
     h = min(len(es[prv]), len(es[nxt])) // 2
@@ -134,8 +125,8 @@ def rank_program(g, core, T, topo):
                                         remote_sem=rs, src=s, dst=o))
         g.remote_dma_fused(tr, local_sem=ls)
 
-    W("g", eHS, eHD)
-    send(T.HS[:, 1, :], T.HL[:, 1, :], T.HS[:, 0, :], T.HL[:, 0, :], sem.hv, sem.hvl)
+    W("g", eWB[0])
+    send(T.WB[:, 0, :], T.HL[:, 1, :], T.WB[:, 1, :], T.HL[:, 0, :], sem.hv, sem.hvl)
     g.wait_ge(sem.im, 32)
     send(T.IMG[:, 512:1024], T.IMG[:, 2560:3072], T.IMG[:, 2048:2560], T.IMG[:, 0:512], sem.hm, sem.hml)
 
@@ -165,9 +156,9 @@ def rank_program(g, core, T, topo):
         W("v", *need)
         return ev(ts(out, src, float(8 - 80 * (i0 + 8)), float(80 * (i1 - i0) - 1), A.add, A.min))
 
-    def lst4(out, src, m, need):
+    def lst4(out, src, m, k, need):
         W("v", need)
-        return ev(*[V.tensor_copy(out[:, 2 * f + b:4 * m:4], src[:, 2 * m * f + b:2 * m * (f + 1):2]) for f in (0, 1) for b in (0, 1)])
+        return ev(*[V.tensor_copy(out[:, b:4 * m:4], src[:, b:k * m:k] if b < k else src[:, k * m + b - k:4 * m:4 - k]) for b in range(4)])
 
     def gat(q, out, win, offs, need, clip=False):
         W(q, *need)
@@ -180,12 +171,14 @@ def rank_program(g, core, T, topo):
     def rows(buf, i0, i1):
         return T[buf][:, 80 * (i0 + 8):80 * (i1 + 8)]
 
-    W("p", eF, eWB, ePD)
+    def blk(buf, i0, c0, c1):
+        return T[buf][:, 80 * (i0 + 8) + 16 * c0:80 * (i0 + 8) + 16 * c1]
+
+    W("p", eF, *eWB)
     eU = []
     for b in range(6):
-        ms = range(3 * b, min(3 * b + 3, 16))
-        eU.append(ev(*[P.matmul(T["P%d" % b][:, 160 * k:160 * k + 160], T.F[:, 2 * (m // 2):2 * (m // 2) + 128],
-                                T.WB[:, 2 * (m % 2):2 * (m % 2) + 2, :], True, True) for k, m in enumerate(ms)]))
+        eU.append(ev(*[P.matmul(T["P%d" % b][:, 80 * k:80 * k + 80], T.F[:, 2 * (i % 8):2 * (i % 8) + 128],
+                                T.WB[:, SLOT[i // 8], :], True, True) for k, i in enumerate(range(6 * b, min(6 * b + 6, 32)))]))
     eC = []
     for b in range(6):
         i0, i1 = 6 * b, min(6 * b + 6, 32)
@@ -194,88 +187,91 @@ def rank_program(g, core, T, topo):
         eC.append(ev(V.tensor_copy(o, i) if b & 1 else S.activation(o, i, AF.Copy)))
     w0a = wrap("S80", [(T.R0[:, 0:16, :], vp("V0", 1, 17))], eS80, *eC[0:3])
     w0b = wrap("S80", [(T.R1[:, 0:14, :], vp("V0", 17, 31))], *eC)
-    KW()
-    K(tt(T.w64[:], T.x0[:], T.t64[:], A.add))
+
+    l0a = lst(T.L0I[:, 0:80], T.R0[:, 0:16, :], 0, 18, w0a)
+    V.wait_ge(sem.kp, 1)
     ePC = ev(ts(T.PC[:], T.PI[:], T.x0[:, 0:1], None, A.mult))
+    need = [l0a] + eC[0:3]
+    gas = gat("s", blk("V1", 1, 0, 42), rows("V0", 0, 18), T.L0I[:, 0:42], need)
+    gav = gat("v", blk("V1", 1, 42, 80), rows("V0", 0, 18), T.L0I[:, 42:80], need)
+    w1a = wrap("S80", [(T.P0[:, 0:60], vp("V1", 3, 15))], gas, gav)
+    l0b = lst(T.L0I[:, 80:150], T.R1[:, 0:14, :], 16, 32, w0b)
+    esh = ev(ts(T.tp[:], T.t64[:], 0.5, None, A.mult), ts(T.tm[:], T.t64[:], -0.5, None, A.mult))
+    need = [l0b] + eC
+    gbs = gat("s", blk("V1", 17, 0, 36), rows("V0", 16, 32), T.L0I[:, 80:116], need)
+    gbv = gat("v", blk("V1", 17, 36, 70), rows("V0", 16, 32), T.L0I[:, 116:150], need)
+    l1a = lst(T.L1I[:, 0:60], T.P0[:, 0:60], 1, 17, w1a)
+    p1i = pads("V1", 1, 31, 2, gas, gav, gbs, gbv, w1a)
+    K(tt(T.w64[:], T.x0[:], T.t64[:], A.add))
     K(ts(T.hi[:], T.x0[:], 63.0 - 1024.0, 1024.0, A.mult, A.add))
     KW()
     eS64 = ev(ts(T.S64[:], T.U[:], T.sc[:, 0:1], T.w64[:, 0:1], A.is_equal, A.mult))
 
-    l0a = lst(T.L0I[:, 0:80], T.R0[:, 0:16, :], 0, 18, w0a)
-    need = [l0a] + eC[0:3]
-    gas = gat("s", rows("V1", 1, 9), rows("V0", 0, 18), T.L0I[:, 0:40], need)
-    gav = gat("v", rows("V1", 9, 17), rows("V0", 0, 18), T.L0I[:, 40:80], need)
-    w1a = wrap("S80", [(T.P0[:, 0:60], vp("V1", 3, 15))], gas, gav)
-    l0b = lst(T.L0I[:, 80:150], T.R1[:, 0:14, :], 16, 32, w0b)
-    need = [l0b] + eC
-    gbs = gat("s", rows("V1", 17, 25), rows("V0", 16, 32), T.L0I[:, 80:120], need)
-    gbv = gat("v", rows("V1", 25, 31), rows("V0", 16, 32), T.L0I[:, 120:150], need)
-    p1i = pads("V1", 1, 31, 2, gas, gav, gbs, gbv, w1a)
-
     def unwrap(bank, part, ks):
         return ev(*[P.matmul(T[bank][:, 80 * j:80 * j + 80], T.F[:, 2 * k:2 * k + 128], T.HL[:, part, :], True, True) for j, k in enumerate(ks)])
     P.wait_ge(sem.hv, 2 * h)
-    eUh = [unwrap("P1", 0, range(1, 5)), unwrap("P3", 1, range(0, 4)), unwrap("P2", 0, range(5, 8)), unwrap("P4", 1, range(4, 7))]
+    eUh = [unwrap("P1", 0, range(1, 5)), unwrap("P2", 0, range(5, 8)), unwrap("P3", 1, range(0, 4)), unwrap("P4", 1, range(4, 7))]
     eCh = []
-    for j, (b, q, i0, i1) in enumerate((("P1", "s", -7, -3), ("P3", "v", 32, 36), ("P2", "s", -3, 0), ("P4", "v", 36, 39))):
-        W(q, eUh[j])
-        o, i = rows("V0", i0, i1), T[b][:, 0:80 * (i1 - i0)]
-        eCh.append(ev(S.activation(o, i, AF.Copy) if q == "s" else V.tensor_copy(o, i)))
-    w0h = wrap("S80", [(T.R0[:, 0:7, :], vp("V0", -6, 1)), (T.R0[:, 7:14, :], vp("V0", 31, 38))], l0a, *eCh)
-    w1b = wrap("S80", [(T.P5[:, 0:70], vp("V1", 15, 29))], p1i)
+    for j, (b, q, sh, i0, i1) in enumerate((("P1", "s", "tm", -7, -3), ("P2", "v", "tm", -3, 0), ("P3", "s", "tp", 32, 36), ("P4", "v", "tp", 36, 39))):
+        W(q, esh, eUh[j])
+        o, i, c = rows("V0", i0, i1), T[b][:, 0:80 * (i1 - i0)], T[sh][:, 0:1]
+        eCh.append(ev(S.activation(o, i, AF.Identity, bias=c) if q == "s" else ts(o, i, c, None, A.add)))
+    w0t = wrap("S80", [(T.R0[:, 0:7, :], vp("V0", -6, 1))], l0a, eCh[0], eCh[1])
+    w0u = wrap("S80", [(T.R1[:, 0:7, :], vp("V0", 31, 38))], l0b, eCh[2], eCh[3])
+    w1b = wrap("S80", [(T.P5[:, 0:80], vp("V1", 15, 31))], p1i)
 
-    l1a = lst(T.L1I[:, 0:60], T.P0[:, 0:60], 1, 17, w1a)
     need = [gas, gav, p1i, l1a]
-    g1s = gat("s", rows("V2", 3, 9), rows("V1", 1, 17), T.L1I[:, 0:30], need)
-    g1v = gat("v", rows("V2", 9, 15), rows("V1", 1, 17), T.L1I[:, 30:60], need)
+    g1s = gat("s", blk("V2", 3, 0, 30), rows("V1", 1, 17), T.L1I[:, 0:30], need)
+    g1v = gat("v", blk("V2", 3, 30, 60), rows("V1", 1, 17), T.L1I[:, 30:60], need)
 
-    l0t = lst(T.L0H[:, 0:35], T.R0[:, 0:7, :], -7, 2, w0h)
-    l0u = lst(T.L0H[:, 36:71], T.R0[:, 7:14, :], 30, 39)
-    need = [l0t, l0u] + eCh
-    h0s = gat("s", rows("V1", -6, 1), rows("V0", -7, 2), T.L0H[:, 0:35], need)
-    h0v = gat("v", rows("V1", 31, 38), rows("V0", 30, 39), T.L0H[:, 36:71], need)
-    l1b = lst(T.L1I[:, 60:130], T.P5[:, 0:70], 13, 31, w1b)
-    p1h = pads("V1", -6, 38, 2, h0s, h0v, w1b, g1s, g1v)
-    w1h = wrap("S80", [(T.P0[:, 0:35], vp("V1", -4, 3)), (T.P0[:, 35:70], vp("V1", 29, 36))], l1a, h0s, h0v, p1h)
+    l0t = lst(T.L0H[:, 0:35], T.R0[:, 0:7, :], -7, 2, w0t)
+    l0u = lst(T.L0H[:, 36:71], T.R1[:, 0:7, :], 30, 39, w0u)
+    h0s = gat("s", rows("V1", -6, 1), rows("V0", -7, 2), T.L0H[:, 0:35], [l0t] + eCh)
+    h0v = gat("v", rows("V1", 31, 37), rows("V0", 30, 39), T.L0H[:, 36:66], [l0u] + eCh)
+    h0w = gat("s", rows("V1", 37, 38), rows("V0", 30, 39), T.L0H[:, 66:71], [l0u] + eCh)
+    l1b = lst(T.L1I[:, 60:140], T.P5[:, 0:80], 13, 33, w1b)
+    p1h = pads("V1", -6, 38, 2, h0s, h0v, h0w, w1b, g1s, g1v)
+    w1t = wrap("S80", [(T.P0[:, 0:35], vp("V1", -4, 3))], l1a, h0s, h0v, h0w, p1h)
+    w1u = wrap("S80", [(T.P3[:, 0:25], vp("V1", 31, 36))])
 
-    need = [gas, gav, gbs, gbv, p1h, l1b]
-    g2s = gat("s", rows("V2", 15, 23), rows("V1", 13, 31), T.L1I[:, 60:100], need)
-    g2v = gat("v", rows("V2", 23, 29), rows("V1", 13, 31), T.L1I[:, 100:130], need)
-    w2i = wrap("S80", [(T.R1[:, 0:18, :], vp("V2", 7, 25, 8))], l0b, g1s, g1v, g2s, g2v)
-    l1t = lst(T.L1H[:, 0:35], T.P0[:, 0:35], -6, 5, w1h)
-    l1u = lst(T.L1H[:, 36:71], T.P0[:, 35:70], 27, 38)
-    need = [l1t, l1u, h0s, h0v, gas, gav, gbs, gbv, p1h]
-    h1s = gat("s", rows("V2", -4, 3), rows("V1", -6, 5), T.L1H[:, 0:35], need)
-    h1v = gat("v", rows("V2", 29, 36), rows("V1", 27, 38), T.L1H[:, 36:71], need)
+    need = [gas, gav, gbs, gbv, h0s, h0v, h0w, p1h, l1b]
+    g2s = gat("s", blk("V2", 15, 0, 44), rows("V1", 13, 33), T.L1I[:, 60:104], need)
+    g2v = gat("v", blk("V2", 15, 44, 80), rows("V1", 13, 33), T.L1I[:, 104:140], need)
+    w2i = wrap("S80", [(T.R1[:, 0:M, :], vp("V2", IO, IO + M, 8))], l0u, g1s, g1v, g2s, g2v)
+    l1t = lst(T.L1H[:, 0:35], T.P0[:, 0:35], -6, 5, w1t)
+    l1u = lst(T.L1H[:, 36:61], T.P3[:, 0:25], 27, 38, w1u)
+    need = [h0s, h0v, h0w, gas, gav, gbs, gbv, p1h]
+    h1s = gat("s", rows("V2", -4, 3), rows("V1", -6, 5), T.L1H[:, 0:35], [l1t] + need)
+    h1v = gat("v", rows("V2", 31, 36), rows("V1", 27, 38), T.L1H[:, 36:61], [l1u] + need)
     p2 = pads("V2", -4, 36, 4, h1s, h1v, g1s, g1v, g2s, g2v, w2i)
-    w2h = wrap("S80", [(T.R0[:, 0:7, :], vp("V2", 0, 7, 8)), (T.R0[:, 7:14, :], vp("V2", 25, 32, 8))], l0t, l0u, h1s, h1v, p2)
+    w2h = wrap("S80", [(T.R0[:, 0:IO, :], vp("V2", 0, IO, 8)), (T.R0[:, IO:2 * IO, :], vp("V2", 32 - IO, 32, 8))], l0t, h1s, h1v, p2)
 
     all2 = [h1s, h1v, g1s, g1v, g2s, g2v, p2]
-    l2l = lst(T.L2IL[:], T.R1[:, 0:18, 0:2], 3, 29, w2i)
-    l2r = lst(T.L2IR[:], T.R1[:, 0:18, 2:4], 3, 29)
-    i2s = gat("s", T.PHI[:, 0:576], rows("V2", 3, 29), T.L2IL[:], [l2l, l2r] + all2, True)
-    i2v = gat("v", T.PHI[:, 576:1152], rows("V2", 3, 29), T.L2IR[:], [l2l, l2r] + all2, True)
-    w3i = wrap("S64", [(T.P1[:, 0:72], lambda q: T.PHI[:, q:1152:16])], eS64, i2s, i2v)
-    l2hl = lst(T.L2HL[:], T.R0[:, 0:14, 0:2], -4, 36, w2h)
-    l2hr = lst(T.L2HR[:], T.R0[:, 0:14, 2:4], -4, 36)
-    h2s = gat("s", T.PHH[:, 0:448], rows("V2", -4, 36), T.L2HL[:], [l2hl, l2hr] + all2, True)
-    h2v = gat("v", T.PHH[:, 448:896], rows("V2", -4, 36), T.L2HR[:], [l2hl, l2hr] + all2, True)
-    w3h = wrap("S64", [(T.P2[:, 0:56], lambda q: T.PHH[:, q:896:16])], h2s, h2v)
+    l2l = lst(T.L2IL[:], T.R1[:, 0:M, 0:2], IO - 4, IO + M + 4, w2i)
+    l2r = lst(T.L2IR[:], T.R1[:, 0:M, 2:4], IO - 4, IO + M + 4)
+    i2s = gat("s", T.PHI[:, 0:32 * M], rows("V2", IO - 4, IO + M + 4), T.L2IL[:], [l2l] + all2, True)
+    i2v = gat("v", T.PHI[:, 32 * M:64 * M], rows("V2", IO - 4, IO + M + 4), T.L2IR[:], [l2r] + all2, True)
+    w3i = wrap("S64", [(T.P1[:, 0:4 * M], lambda q: T.PHI[:, q:64 * M:16])], eS64, i2s, i2v)
+    l2hl = lst(T.L2HL[:], T.R0[:, 0:2 * IO, 0:3], -4, 36, w2h)
+    l2hr = lst(T.L2HR[:], T.R0[:, 0:2 * IO, 3:4], -4, 36)
+    h2s = gat("s", T.PHH[:, 0:96 * IO], rows("V2", -4, 36), T.L2HL[:], [l2hl] + all2, True)
+    h2v = gat("v", T.PHH[:, 96 * IO:128 * IO], rows("V2", -4, 36), T.L2HR[:], [l2hr] + all2, True)
+    w3h = wrap("S64", [(T.P2[:, 0:8 * IO], lambda q: T.PHH[:, q:128 * IO:16])], h2s, h2v)
 
-    l3i = lst4(T.L3I, T.P1, 18, w3i)
+    l3i = lst4(T.L3I, T.P1, M, 2, w3i)
     for q in (V, S):
         q.wait_ge(sem.im, 32)
         q.wait_ge(sem.imm, 16)
         q.wait_ge(sem.hm, 2 * h)
     a3 = 10
-    yi, ym, yj = 7 * 64, (7 + a3) * 64, 25 * 64
+    yi, ym, yj = IO * 64, (IO + a3) * 64, (IO + M) * 64
     g3s = gat("s", T.Y[:, yi:ym], T.IMG[:], T.L3I[:, 0:4 * a3], [l3i])
-    g3v = gat("v", T.Y[:, ym:yj], T.IMG[:], T.L3I[:, 4 * a3:72], [l3i])
+    g3v = gat("v", T.Y[:, ym:yj], T.IMG[:], T.L3I[:, 4 * a3:4 * M], [l3i])
     W("y", g3s, g3v)
     Y.dma_start(out=T.y[:, yi:yj], in_=T.Y[:, yi:yj]).then_inc(sem.sto, 16)
-    l3h = lst4(T.L3H, T.P2, 14, w3h)
-    h3s = gat("s", T.Y[:, 0:yi], T.IMG[:], T.L3H[:, 0:28], [l3h])
-    h3v = gat("v", T.Y[:, yj:2048], T.IMG[:], T.L3H[:, 28:56], [l3h])
+    l3h = lst4(T.L3H, T.P2, 2 * IO, 3, w3h)
+    h3s = gat("s", T.Y[:, 0:yi], T.IMG[:], T.L3H[:, 0:4 * IO], [l3h])
+    h3v = gat("v", T.Y[:, yj:2048], T.IMG[:], T.L3H[:, 4 * IO:8 * IO], [l3h])
     W("s", h3s)
     S.dma_start(out=T.y[:, 0:yi], in_=T.Y[:, 0:yi]).then_inc(sem.sto, 16)
     W("y", h3v)

@@ -5,31 +5,38 @@ import comms_topo
 A = AluOpType
 AF = ActivationFunctionType
 B16, F32, I32, U16 = "bfloat16", "float32", "int32", "uint16"
-IO = 6
+IO = 7
 M = 32 - 2 * IO
+G = 15
+NA, NB = 5 * (G - 3), 5 * (29 - G)
+KL = 3
+CA, CB, C1, C2, D1, A3 = 46, 36, 30, 42, 34, 10
 
 
 def bufs():
     d = {}
     for names, shape, ty in (
-            ("b15 m16", [128, 1], I32), ("K4 t7 RR", [128, 4], I32), ("U", [128, 144], F32), ("PI PC", [128, 16], F32),
-            ("BW", [128, 4, 2], F32), ("fc xf sc x0 tp tm t80 t64 w80 w64 hi", [128, 1], F32), ("tc", [128, 4], F32),
-            ("F S80 S64", [128, 144], B16), ("WV", [128, 4, 64], I32), ("WB", [128, 4, 80], B16),
-            ("HL", [128, 2, 80], B16), ("V0 V1 V2", [128, 3840], B16),
+            ("b15 m16", [128, 1], I32), ("K1 K2", [128, 2], I32), ("KR", [128, 4], I32), ("RR tc", [128, 4], F32),
+            ("U", [128, 144], F32), ("PI PC", [128, 16], F32),
+            ("kf xf sc x0 t80 t64 w80 w64 hi", [128, 1], F32),
+            ("S80 S64", [128, 144], B16), ("SD", [128, 64], B16), ("WV", [128, 6, 64], I32), ("WB", [128, 6, 80], B16),
+            ("WL", [128, 2, 5, 32], B16), ("HL", [128, 2, 80], B16), ("V0 V1 V2", [128, 3840], B16),
             ("PHI", [128, 64 * M], B16), ("PHH", [128, 128 * IO], B16), ("L0I", [128, 150], U16), ("L1I", [128, 140], U16),
-            ("L0H L1H", [128, 72], U16), ("L2IL L2IR", [128, 2 * M], U16), ("L2HL", [128, 6 * IO], U16), ("L2HR", [128, 2 * IO], U16),
+            ("SL", [128, 60], U16), ("LT LD", [128, 30], U16), ("LX", [128, 12], U16),
+            ("L1H", [128, 76], U16), ("L2IL L2IR", [128, 2 * M], U16), ("L2HL L2HR", [128, 6 * IO], U16),
             ("L3I", [128, 4 * M], U16), ("L3H", [128, 8 * IO], U16), ("IMG", [128, 3072], B16), ("Y", [128, 2048], B16)):
         for nm in names.split():
             d[nm] = ("sbuf", shape, ty)
-    for nm in "P0 P1 P2 P3 P4 P5".split():
+    for nm in "P0 P1 P2 P4".split():
         d[nm] = ("psum", [128, 512], F32)
     for nm in "R0 R1".split():
         d[nm] = ("psum", [128, 102, 5], F32)
+    d["TB"] = ("psum", [128, 6, 80], F32)
     return d
 
 
 SCRATCH = bufs()
-SEMAPHORES = ["oa", "ow", "im", "imm", "hv", "hvl", "hm", "hml", "sto", "kc", "kg", "kh", "kp"] + ["e%d" % i for i in range(120)]
+SEMAPHORES = ["od", "oh", "im", "imm", "hv", "hvl", "hm", "hml", "hl", "hll", "sto", "kc", "kg", "kh", "kp", "kq", "ks", "vo", "vh"] + ["e%d" % i for i in range(100)]
 
 
 def rank_program(g, core, T, topo):
@@ -57,18 +64,31 @@ def rank_program(g, core, T, topo):
                 seen[(q, e)] = 1
                 Q[q].wait_ge(sem[e], total[e])
 
-    SLOT = (0, 2, 3, 1)
-    for r in (0, 3, 1, 2):
-        sm = sem.oa if r in (0, 3) else sem.ow
-        Y.dma_start(out=T.WV[0:64, SLOT[r], :], in_=T.vx[:, 512 * r:512 * r + 512]).then_inc(sm, 16)
-        S.dma_start(out=T.WV[64:128, SLOT[r], :], in_=T.vy[:, 512 * r:512 * r + 512]).then_inc(sm, 16)
+    def WD(q, s, v):
+        if (q, s) not in seen:
+            seen[(q, s)] = 1
+            Q[q].wait_ge(sem[s], v)
+
+    for b in (0, 1):
+        Y.dma_start(out=T.WV[0:64, 2 * b:2 * b + 2, :], in_=T.vx[b::2, :]).then_inc(sem.od, 16)
+        S.dma_start(out=T.WV[64:128, 2 * b:2 * b + 2, :], in_=T.vy[b::2, :]).then_inc(sem.od, 16)
+    for b, a in ((4, 0), (5, 1536)):
+        Y.dma_start(out=T.WV[0:64, b, :], in_=T.vx[:, a:a + 512]).then_inc(sem.oh, 16)
+        S.dma_start(out=T.WV[64:128, b, :], in_=T.vy[:, a:a + 512]).then_inc(sem.oh, 16)
     Y.dma_start(out=T.IMG[:, 512:1024], in_=T.img[:, 0:512]).then_inc(sem.im, 16)
     S.dma_start(out=T.IMG[:, 2048:2560], in_=T.img[:, 1536:2048]).then_inc(sem.im, 16)
     Y.dma_start(out=T.IMG[:, 1024:2048], in_=T.img[:, 512:1536]).then_inc(sem.imm, 16)
 
-    for o, pat, b0, cm, sm in ((T.K4, [[0, 4]], 0, 1, sem.kg), (T.RR, [[8, 4]], 8, 0, sem.kg), (T.U, [[1, 144]], 0, 0, sem.kh),
-                               (T.PI, [[9, 2], [1, 8]], -8, 0, sem.kp)):
-        g.iota(o[:], pat, b0, cm, allow_small_or_imprecise_dtypes=True).then_inc(sm, 1)
+    def iota(o, pat, b0, cm, sm):
+        g.iota(o, pat, b0, cm, allow_small_or_imprecise_dtypes=True).then_inc(sm, 1)
+
+    iota(T.K2[:], [[1, 2]], 0, 2, sem.kg)
+    iota(T.K1[:], [[0, 2]], 0, 1, sem.kg)
+    iota(T.RR[:, 0:2], [[0, 2]], 8, 0, sem.kg)
+    iota(T.RR[:, 2:4], [[-40, 2]], 40, 0, sem.kg)
+    iota(T.U[:], [[1, 144]], 0, 0, sem.kh)
+    iota(T.kf[:], [[0, 1]], 0, 1, sem.ks)
+    iota(T.V0[:, 2800:3200], [[0, 400]], 0, 0, sem.kp)
     kc = [0]
 
     def K(ins):
@@ -79,40 +99,36 @@ def rank_program(g, core, T, topo):
         V.wait_ge(sem.kc, kc[0])
 
     ts, tt = V.tensor_scalar, V.tensor_tensor
-    e0 = ev(V.memset(T.tc[0:64, :], 0.0))
+    e0 = ev(V.memset(T.tc[0:64, :], -1.0))
+    eZa = ev(V.memset(T.V0[:, 0:640], 0.0))
     K(V.memset(T.WB[:], 0.0))
-    V.wait_ge(sem.kg, 2)
-    K(ts(T.t7[:], T.K4[:], 7, None, A.bitwise_and))
-    exf = ev(ts(T.xf[:], T.K4[:, 0:1], 64.0, None, A.is_lt))
-    K(ts(T.fc[0:64, :], T.K4[0:64, 0:1], 2.0, None, A.mult))
-    K(ts(T.fc[64:128, :], T.K4[64:128, 0:1], 2.0, -127.0, A.mult, A.add))
+    V.wait_ge(sem.kg, 4)
+    K(ts(T.KR[:, 0:2], T.K2[:], 31, None, A.bitwise_and))
+    K(ts(T.KR[:, 2:4], T.K1[:], 7, None, A.bitwise_and))
+    exf = ev(ts(T.xf[:], T.K1[:, 0:1], 64.0, None, A.is_lt))
     KW()
-    etc = ev(tt(T.tc[64:128, :], T.t7[64:128, :], T.RR[64:128, :], A.add))
-    V.wait_ge(sem.kh, 1)
-    eF = ev(ts(T.F[:], T.U[:], T.fc[:, 0:1], None, A.is_equal))
+    etc = ev(tt(T.tc[64:128, :], T.KR[64:128, :], T.RR[64:128, :], A.add))
+    eZ = ev(V.memset(T.V0[:, 1200:2800], 0.0))
+    W("s", eZa)
+    eZb = ev(S.activation(T.V0[:, 640:1200], T.V0[:, 0:560], AF.Copy))
     S.wait_ge(sem.kh, 1)
     W("s", e0, exf, etc)
-    ebw = ev(*[S.activation(T.P5[:, 64 * SLOT[r]:64 * SLOT[r] + 64], T.U[:, 0:64], AF.Identity, bias=T.tc[:, r:r + 1], scale=T.xf[:, 0:1]) for r in range(4)])
-    W("v", exf, ebw)
-    K(ts(T.BW[:, :, 0], T.P5[:, 0:256:64], T.xf[:, 0:1], None, A.subtract))
-    K(ts(T.BW[:, :, 1], T.P5[:, 63:256:64], T.xf[:, 0:1], None, A.add))
+    etb = ev(*[S.activation(T.TB[:, s, 0:66], T.U[:, 0:66], AF.Identity, bias=T.tc[:, r:r + 1], scale=T.xf[:, 0:1])
+               for s, r in enumerate((0, 1, 0, 1, 2, 3))])
     KW()
-    eWB = []
-    for sm, a in ((sem.oa, 0), (sem.ow, 2)):
-        V.wait_ge(sm, 64)
-        eWB.append(ev(tt(T.WB[:, a:a + 2, 8:72], T.WV[:, a:a + 2, :], T.P5[:, 64 * a:64 * a + 128], A.add),
-                      tt(T.WB[:, a:a + 2, 7:73:65], T.WV[:, a:a + 2, 0:64:63], T.BW[:, a:a + 2, :], A.add)))
-    K(ts(T.b15[:], T.K4[:, 0:1], 15, None, A.bitwise_and))
-    K(ts(T.m16[:], T.K4[:, 0:1], 112, None, A.bitwise_and))
-    KW()
-    K(ts(T.x0[:], T.b15[:], 0.0, None, A.is_equal))
-    K(ts(T.t80[:], T.b15[:], 1.0, 80.0, A.is_equal, A.mult))
-    K(ts(T.sc[:], T.m16[:], 15.0, None, A.add))
-    KW()
-    K(tt(T.w80[:], T.x0[:], T.t80[:], A.add))
-    K(ts(T.t64[:], T.b15[:], 1.0, 64.0, A.is_equal, A.mult))
-    KW()
-    eS80 = ev(ts(T.S80[:], T.U[:], T.sc[:, 0:1], T.w80[:, 0:1], A.is_equal, A.mult))
+    V.wait_ge(sem.od, 64)
+    V.wait_ge(sem.oh, 64)
+    W("v", etb)
+    eWB = ev(tt(T.WB[:, :, 8:72], T.WV[:], T.TB[:, :, 1:65], A.add),
+             tt(T.WB[:, :, 7:73:65], T.WV[:, :, 0:64:63], T.TB[:, :, 0:66:65], A.add))
+    for part, q in ((0, "y"), (1, "s")):
+        W(q, eZ, eZb, eWB)
+        Q[q].wait_ge(sem.kp, 1)
+        for b in (0, 1):
+            Q[q].dma_start(out=T.V0[16 * b + part::32, 640:3200], in_=T.WB[64 * part:64 * part + 64, 2 * b:2 * b + 2, :]).then_inc(sem.vo, 16)
+    W("v", eWB)
+    eWL = ev(V.tensor_copy(T.WL[:, :, :, 0:16], T.WB[:, 0:2, :]), S.activation(T.WL[:, :, :, 16:32], T.WB[:, 2:4, :], AF.Copy))
+    eZh = ev(S.activation(T.V0[:, 3200:3840], T.V0[:, 0:640], AF.Copy))
 
     es = {d: topo.engines(core, d) for d in (prv, nxt)}
     h = min(len(es[prv]), len(es[nxt])) // 2
@@ -125,10 +141,27 @@ def rank_program(g, core, T, topo):
                                         remote_sem=rs, src=s, dst=o))
         g.remote_dma_fused(tr, local_sem=ls)
 
-    W("g", eWB[0])
-    send(T.WB[:, 0, :], T.HL[:, 1, :], T.WB[:, 1, :], T.HL[:, 0, :], sem.hv, sem.hvl)
-    g.wait_ge(sem.im, 32)
-    send(T.IMG[:, 512:1024], T.IMG[:, 2560:3072], T.IMG[:, 2048:2560], T.IMG[:, 0:512], sem.hm, sem.hml)
+    W("g", eWB)
+    send(T.WB[:, 4, :], T.HL[:, 1, :], T.WB[:, 5, :], T.HL[:, 0, :], sem.hv, sem.hvl)
+    iota(T.PI[:], [[9, 2], [1, 8]], -8, 0, sem.kq)
+
+    W("y", eZa, eZh)
+    Y.wait_ge(sem.hv, 2 * h)
+    for side, a in ((0, 0), (1, 3200)):
+        for part in (0, 1):
+            Y.dma_start(out=T.V0[part::16, a:a + 640], in_=T.HL[64 * part:64 * part + 64, side, :]).then_inc(sem.vh, 16)
+
+    V.wait_ge(sem.kh, 1)
+    V.wait_ge(sem.ks, 1)
+    eSD = ev(ts(T.SD[0:64, :], T.U[0:64, 0:64], T.kf[0:64, 0:1], 1.0, A.is_equal, A.mult),
+             ts(T.SD[64:128, :], T.U[64:128, 64:128], T.kf[64:128, 0:1], 80.0, A.is_equal, A.mult))
+    K(ts(T.b15[:], T.K1[:, 0:1], 15, None, A.bitwise_and))
+    K(ts(T.m16[:], T.K1[:, 0:1], 112, None, A.bitwise_and))
+    KW()
+    K(ts(T.x0[:], T.b15[:], 0.0, None, A.is_equal))
+    K(ts(T.t80[:], T.b15[:], 1.0, 80.0, A.is_equal, A.mult))
+    K(ts(T.sc[:], T.m16[:], 15.0, None, A.add))
+    KW()
 
     def pads(buf, i0, i1, w, *need):
         W("s", ePC, *need)
@@ -174,88 +207,75 @@ def rank_program(g, core, T, topo):
     def blk(buf, i0, c0, c1):
         return T[buf][:, 80 * (i0 + 8) + 16 * c0:80 * (i0 + 8) + 16 * c1]
 
-    W("p", eF, *eWB)
-    eU = []
-    for b in range(6):
-        eU.append(ev(*[P.matmul(T["P%d" % b][:, 80 * k:80 * k + 80], T.F[:, 2 * (i % 8):2 * (i % 8) + 128],
-                                T.WB[:, SLOT[i // 8], :], True, True) for k, i in enumerate(range(6 * b, min(6 * b + 6, 32)))]))
-    eC = []
-    for b in range(6):
-        i0, i1 = 6 * b, min(6 * b + 6, 32)
-        o, i = rows("V0", i0, i1), T["P%d" % b][:, 0:80 * (i1 - i0)]
-        W("sv"[b & 1], eU[b])
-        eC.append(ev(V.tensor_copy(o, i) if b & 1 else S.activation(o, i, AF.Copy)))
-    w0a = wrap("S80", [(T.R0[:, 0:16, :], vp("V0", 1, 17))], eS80, *eC[0:3])
-    w0b = wrap("S80", [(T.R1[:, 0:14, :], vp("V0", 17, 31))], *eC)
+    W("p", eSD, eWL)
+    w0 = ev(*[P.matmul(T.R0[32 * k:32 * k + 32, i:32:2, b], T.WL[:, i, b, :], T.SD[:, 16 * k:16 * k + 16], True, True)
+              for b in range(5) for i in (0, 1) for k in range(4)])
+    l0a = lst(T.L0I[:], T.R0[:, 1:31, :], 0, 32, w0)
+    esl = ev(ts(T.SL[:, 0:30], T.R0[:, 0:6, :], 8.0 + 2560.0, 3839.0, A.add, A.min),
+             ts(T.SL[:, 30:60], T.R0[:, 26:32, :], 8.0 - 2560.0, 3839.0, A.add, A.min))
+    W("g", esl)
+    send(T.SL[:, 0:30], T.LD[:], T.SL[:, 30:60], T.LT[:], sem.hl, sem.hll)
+    g.wait_ge(sem.im, 32)
+    send(T.IMG[:, 512:1024], T.IMG[:, 2560:3072], T.IMG[:, 2048:2560], T.IMG[:, 0:512], sem.hm, sem.hml)
+    lx = ev(*[ts(T.LX[:, 6 * k:6 * k + 5], T.R0[:, 31 * k, :], 8.0, 3839.0, A.add, A.min) for k in (0, 1)])
+    K(tt(T.w80[:], T.x0[:], T.t80[:], A.add))
+    K(ts(T.t64[:], T.b15[:], 1.0, 64.0, A.is_equal, A.mult))
 
-    l0a = lst(T.L0I[:, 0:80], T.R0[:, 0:16, :], 0, 18, w0a)
-    V.wait_ge(sem.kp, 1)
+    for q in "vs":
+        WD(q, "vo", 64)
+    gas = gat("s", blk("V1", 1, 0, CA), rows("V0", 0, 32), T.L0I[:, 0:CA], [l0a])
+    gav = gat("v", blk("V1", 1, CA, 80), rows("V0", 0, 32), T.L0I[:, CA:80], [l0a])
+    KW()
+    eS80 = ev(ts(T.S80[:], T.U[:], T.sc[:, 0:1], T.w80[:, 0:1], A.is_equal, A.mult))
+    V.wait_ge(sem.kq, 1)
     ePC = ev(ts(T.PC[:], T.PI[:], T.x0[:, 0:1], None, A.mult))
-    need = [l0a] + eC[0:3]
-    gas = gat("s", blk("V1", 1, 0, 42), rows("V0", 0, 18), T.L0I[:, 0:42], need)
-    gav = gat("v", blk("V1", 1, 42, 80), rows("V0", 0, 18), T.L0I[:, 42:80], need)
-    w1a = wrap("S80", [(T.P0[:, 0:60], vp("V1", 3, 15))], gas, gav)
-    l0b = lst(T.L0I[:, 80:150], T.R1[:, 0:14, :], 16, 32, w0b)
-    esh = ev(ts(T.tp[:], T.t64[:], 0.5, None, A.mult), ts(T.tm[:], T.t64[:], -0.5, None, A.mult))
-    need = [l0b] + eC
-    gbs = gat("s", blk("V1", 17, 0, 36), rows("V0", 16, 32), T.L0I[:, 80:116], need)
-    gbv = gat("v", blk("V1", 17, 36, 70), rows("V0", 16, 32), T.L0I[:, 116:150], need)
-    l1a = lst(T.L1I[:, 0:60], T.P0[:, 0:60], 1, 17, w1a)
+    w1a = wrap("S80", [(T.P0[:, 0:NA], vp("V1", 3, G))], eS80, gas, gav)
+    gbs = gat("s", blk("V1", 17, 0, CB), rows("V0", 0, 32), T.L0I[:, 80:80 + CB], [l0a])
+    gbv = gat("v", blk("V1", 17, CB, 70), rows("V0", 0, 32), T.L0I[:, 80 + CB:150], [l0a])
+    l1a = lst(T.L1I[:, 0:NA], T.P0[:, 0:NA], 1, G + 2, w1a)
     p1i = pads("V1", 1, 31, 2, gas, gav, gbs, gbv, w1a)
+    in1 = [gas, gav, gbs, gbv, p1i]
+
+    w1b = wrap("S80", [(T.P4[:, 0:NB], vp("V1", G, 29))], p1i)
+    g1s = gat("s", blk("V2", 3, 0, C1), rows("V1", 1, G + 2), T.L1I[:, 0:C1], in1 + [l1a])
+    g1v = gat("v", blk("V2", 3, C1, NA), rows("V1", 1, G + 2), T.L1I[:, C1:NA], in1 + [l1a])
+
+    for q in "vs":
+        WD(q, "vh", 64)
+        WD(q, "hl", 2 * h)
+    h0s = gat("s", rows("V1", -6, 0), T.V0[:], T.LT[:], [])
+    h0v = gat("v", rows("V1", 32, 38), T.V0[:], T.LD[:], [])
+    h0w = gat("s", rows("V1", 0, 1), T.V0[:], T.LX[:, 0:5], [lx])
+    h0x = gat("v", rows("V1", 31, 32), T.V0[:], T.LX[:, 6:11], [lx])
+    l1b = lst(T.L1I[:, 70:70 + NB], T.P4[:, 0:NB], G - 2, 31, w1b)
+    p1h = pads("V1", -6, 38, 2, h0s, h0v, h0w, h0x, w1b, g1s, g1v)
+    all1 = in1 + [h0s, h0v, h0w, h0x, p1h]
+    w1h = wrap("S80", [(T.P0[:, 0:40], vp("V1", -4, 4)), (T.P0[:, 40:75], vp("V1", 29, 36))], l1a, *all1)
+
+    g2s = gat("s", blk("V2", G, 0, C2), rows("V1", G - 2, 31), T.L1I[:, 70:70 + C2], all1 + [l1b])
+    g2v = gat("v", blk("V2", G, C2, NB), rows("V1", G - 2, 31), T.L1I[:, 70 + C2:70 + NB], all1 + [l1b])
+    w2i = wrap("S80", [(T.R1[:, 0:M, :], vp("V2", IO, IO + M, 8))], g1s, g1v, g2s, g2v)
     K(tt(T.w64[:], T.x0[:], T.t64[:], A.add))
     K(ts(T.hi[:], T.x0[:], 63.0 - 1024.0, 1024.0, A.mult, A.add))
     KW()
-    eS64 = ev(ts(T.S64[:], T.U[:], T.sc[:, 0:1], T.w64[:, 0:1], A.is_equal, A.mult))
+    l1h = lst(T.L1H[:, 0:75], T.P0[:, 0:75], -6, 38, w1h)
+    h1s = gat("s", rows("V2", -4, 3), rows("V1", -6, 38), T.L1H[:, 0:35], all1 + [l1h])
+    h1v = gat("v", blk("V2", 29, 0, D1), rows("V1", -6, 38), T.L1H[:, 40:40 + D1], all1 + [l1h])
+    h1w = gat("s", blk("V2", 29, D1, 35), rows("V1", -6, 38), T.L1H[:, 40 + D1:75], all1 + [l1h])
+    p2 = pads("V2", -4, 36, 4, h1s, h1v, h1w, g1s, g1v, g2s, g2v, w2i)
+    all2 = [h1s, h1v, h1w, g1s, g1v, g2s, g2v, p2]
+    w2h = wrap("S80", [(T.R0[:, 0:IO, :], vp("V2", 0, IO, 8)), (T.R0[:, IO:2 * IO, :], vp("V2", 32 - IO, 32, 8))], l0a, esl, lx, *all2)
 
-    def unwrap(bank, part, ks):
-        return ev(*[P.matmul(T[bank][:, 80 * j:80 * j + 80], T.F[:, 2 * k:2 * k + 128], T.HL[:, part, :], True, True) for j, k in enumerate(ks)])
-    P.wait_ge(sem.hv, 2 * h)
-    eUh = [unwrap("P1", 0, range(1, 5)), unwrap("P2", 0, range(5, 8)), unwrap("P3", 1, range(0, 4)), unwrap("P4", 1, range(4, 7))]
-    eCh = []
-    for j, (b, q, sh, i0, i1) in enumerate((("P1", "s", "tm", -7, -3), ("P2", "v", "tm", -3, 0), ("P3", "s", "tp", 32, 36), ("P4", "v", "tp", 36, 39))):
-        W(q, esh, eUh[j])
-        o, i, c = rows("V0", i0, i1), T[b][:, 0:80 * (i1 - i0)], T[sh][:, 0:1]
-        eCh.append(ev(S.activation(o, i, AF.Identity, bias=c) if q == "s" else ts(o, i, c, None, A.add)))
-    w0t = wrap("S80", [(T.R0[:, 0:7, :], vp("V0", -6, 1))], l0a, eCh[0], eCh[1])
-    w0u = wrap("S80", [(T.R1[:, 0:7, :], vp("V0", 31, 38))], l0b, eCh[2], eCh[3])
-    w1b = wrap("S80", [(T.P5[:, 0:80], vp("V1", 15, 31))], p1i)
-
-    need = [gas, gav, p1i, l1a]
-    g1s = gat("s", blk("V2", 3, 0, 30), rows("V1", 1, 17), T.L1I[:, 0:30], need)
-    g1v = gat("v", blk("V2", 3, 30, 60), rows("V1", 1, 17), T.L1I[:, 30:60], need)
-
-    l0t = lst(T.L0H[:, 0:35], T.R0[:, 0:7, :], -7, 2, w0t)
-    l0u = lst(T.L0H[:, 36:71], T.R1[:, 0:7, :], 30, 39, w0u)
-    h0s = gat("s", rows("V1", -6, 1), rows("V0", -7, 2), T.L0H[:, 0:35], [l0t] + eCh)
-    h0v = gat("v", rows("V1", 31, 37), rows("V0", 30, 39), T.L0H[:, 36:66], [l0u] + eCh)
-    h0w = gat("s", rows("V1", 37, 38), rows("V0", 30, 39), T.L0H[:, 66:71], [l0u] + eCh)
-    l1b = lst(T.L1I[:, 60:140], T.P5[:, 0:80], 13, 33, w1b)
-    p1h = pads("V1", -6, 38, 2, h0s, h0v, h0w, w1b, g1s, g1v)
-    w1t = wrap("S80", [(T.P0[:, 0:35], vp("V1", -4, 3))], l1a, h0s, h0v, h0w, p1h)
-    w1u = wrap("S80", [(T.P3[:, 0:25], vp("V1", 31, 36))])
-
-    need = [gas, gav, gbs, gbv, h0s, h0v, h0w, p1h, l1b]
-    g2s = gat("s", blk("V2", 15, 0, 44), rows("V1", 13, 33), T.L1I[:, 60:104], need)
-    g2v = gat("v", blk("V2", 15, 44, 80), rows("V1", 13, 33), T.L1I[:, 104:140], need)
-    w2i = wrap("S80", [(T.R1[:, 0:M, :], vp("V2", IO, IO + M, 8))], l0u, g1s, g1v, g2s, g2v)
-    l1t = lst(T.L1H[:, 0:35], T.P0[:, 0:35], -6, 5, w1t)
-    l1u = lst(T.L1H[:, 36:61], T.P3[:, 0:25], 27, 38, w1u)
-    need = [h0s, h0v, h0w, gas, gav, gbs, gbv, p1h]
-    h1s = gat("s", rows("V2", -4, 3), rows("V1", -6, 5), T.L1H[:, 0:35], [l1t] + need)
-    h1v = gat("v", rows("V2", 31, 36), rows("V1", 27, 38), T.L1H[:, 36:61], [l1u] + need)
-    p2 = pads("V2", -4, 36, 4, h1s, h1v, g1s, g1v, g2s, g2v, w2i)
-    w2h = wrap("S80", [(T.R0[:, 0:IO, :], vp("V2", 0, IO, 8)), (T.R0[:, IO:2 * IO, :], vp("V2", 32 - IO, 32, 8))], l0t, h1s, h1v, p2)
-
-    all2 = [h1s, h1v, g1s, g1v, g2s, g2v, p2]
     l2l = lst(T.L2IL[:], T.R1[:, 0:M, 0:2], IO - 4, IO + M + 4, w2i)
     l2r = lst(T.L2IR[:], T.R1[:, 0:M, 2:4], IO - 4, IO + M + 4)
-    i2s = gat("s", T.PHI[:, 0:32 * M], rows("V2", IO - 4, IO + M + 4), T.L2IL[:], [l2l] + all2, True)
-    i2v = gat("v", T.PHI[:, 32 * M:64 * M], rows("V2", IO - 4, IO + M + 4), T.L2IR[:], [l2r] + all2, True)
+    i2s = gat("s", T.PHI[:, 0:32 * M], rows("V2", IO - 4, IO + M + 4), T.L2IL[:], all2 + [l2l], True)
+    i2v = gat("v", T.PHI[:, 32 * M:64 * M], rows("V2", IO - 4, IO + M + 4), T.L2IR[:], all2 + [l2r], True)
+    eS64 = ev(ts(T.S64[:], T.U[:], T.sc[:, 0:1], T.w64[:, 0:1], A.is_equal, A.mult))
     w3i = wrap("S64", [(T.P1[:, 0:4 * M], lambda q: T.PHI[:, q:64 * M:16])], eS64, i2s, i2v)
-    l2hl = lst(T.L2HL[:], T.R0[:, 0:2 * IO, 0:3], -4, 36, w2h)
-    l2hr = lst(T.L2HR[:], T.R0[:, 0:2 * IO, 3:4], -4, 36)
-    h2s = gat("s", T.PHH[:, 0:96 * IO], rows("V2", -4, 36), T.L2HL[:], [l2hl] + all2, True)
-    h2v = gat("v", T.PHH[:, 96 * IO:128 * IO], rows("V2", -4, 36), T.L2HR[:], [l2hr] + all2, True)
+    l2hl = lst(T.L2HL[:, 0:2 * IO * KL], T.R0[:, 0:2 * IO, 0:KL], -4, 36, w2h)
+    l2hr = lst(T.L2HR[:, 0:2 * IO * (4 - KL)], T.R0[:, 0:2 * IO, KL:4], -4, 36)
+    h2s = gat("s", T.PHH[:, 0:32 * IO * KL], rows("V2", -4, 36), T.L2HL[:, 0:2 * IO * KL], all2 + [l2hl], True)
+    h2v = gat("v", T.PHH[:, 32 * IO * KL:128 * IO], rows("V2", -4, 36), T.L2HR[:, 0:2 * IO * (4 - KL)], all2 + [l2hr], True)
     w3h = wrap("S64", [(T.P2[:, 0:8 * IO], lambda q: T.PHH[:, q:128 * IO:16])], h2s, h2v)
 
     l3i = lst4(T.L3I, T.P1, M, 2, w3i)
@@ -263,13 +283,13 @@ def rank_program(g, core, T, topo):
         q.wait_ge(sem.im, 32)
         q.wait_ge(sem.imm, 16)
         q.wait_ge(sem.hm, 2 * h)
-    a3 = 10
-    yi, ym, yj = IO * 64, (IO + a3) * 64, (IO + M) * 64
-    g3s = gat("s", T.Y[:, yi:ym], T.IMG[:], T.L3I[:, 0:4 * a3], [l3i])
-    g3v = gat("v", T.Y[:, ym:yj], T.IMG[:], T.L3I[:, 4 * a3:4 * M], [l3i])
+    yi, ym, yj = IO * 64, (IO + A3) * 64, (IO + M) * 64
+    g3s = gat("s", T.Y[:, yi:ym], T.IMG[:], T.L3I[:, 0:4 * A3], [l3i])
+    g3v = gat("v", T.Y[:, ym:yj], T.IMG[:], T.L3I[:, 4 * A3:4 * M], [l3i])
     W("y", g3s, g3v)
     Y.dma_start(out=T.y[:, yi:yj], in_=T.Y[:, yi:yj]).then_inc(sem.sto, 16)
-    l3h = lst4(T.L3H, T.P2, 2 * IO, 3, w3h)
+
+    l3h = lst4(T.L3H, T.P2, 2 * IO, KL, w3h)
     h3s = gat("s", T.Y[:, 0:yi], T.IMG[:], T.L3H[:, 0:4 * IO], [l3h])
     h3v = gat("v", T.Y[:, yj:2048], T.IMG[:], T.L3H[:, 4 * IO:8 * IO], [l3h])
     W("s", h3s)
@@ -280,3 +300,4 @@ def rank_program(g, core, T, topo):
     Y.wait_ge(sem.sto, 48)
     g.wait_ge(sem.hvl, 2 * h)
     g.wait_ge(sem.hml, 2 * h)
+    g.wait_ge(sem.hll, 2 * h)

from concourse.bass import DstId, RemoteDMATransfer
from concourse.mybir import AluOpType, ActivationFunctionType
import comms_topo

A = AluOpType
AF = ActivationFunctionType
B16, F32, I32, U16 = "bfloat16", "float32", "int32", "uint16"
IO = 7
M = 32 - 2 * IO
G = 15
NA, NB = 5 * (G - 3), 5 * (29 - G)
KL = 3
CA, CB, C1, C2, D1, A3 = 46, 36, 30, 42, 34, 10


def bufs():
    d = {}
    for names, shape, ty in (
            ("b15 m16", [128, 1], I32), ("K1 K2", [128, 2], I32), ("KR", [128, 4], I32), ("RR tc", [128, 4], F32),
            ("U", [128, 144], F32), ("PI PC", [128, 16], F32),
            ("kf xf sc x0 t80 t64 w80 w64 hi", [128, 1], F32),
            ("S80 S64", [128, 144], B16), ("SD", [128, 64], B16), ("WV", [128, 6, 64], I32), ("WB", [128, 6, 80], B16),
            ("WL", [128, 2, 5, 32], B16), ("HL", [128, 2, 80], B16), ("V0 V1 V2", [128, 3840], B16),
            ("PHI", [128, 64 * M], B16), ("PHH", [128, 128 * IO], B16), ("L0I", [128, 150], U16), ("L1I", [128, 140], U16),
            ("SL", [128, 60], U16), ("LT LD", [128, 30], U16), ("LX", [128, 12], U16),
            ("L1H", [128, 76], U16), ("L2IL L2IR", [128, 2 * M], U16), ("L2HL L2HR", [128, 6 * IO], U16),
            ("L3I", [128, 4 * M], U16), ("L3H", [128, 8 * IO], U16), ("IMG", [128, 3072], B16), ("Y", [128, 2048], B16)):
        for nm in names.split():
            d[nm] = ("sbuf", shape, ty)
    for nm in "P0 P1 P2 P4".split():
        d[nm] = ("psum", [128, 512], F32)
    for nm in "R0 R1".split():
        d[nm] = ("psum", [128, 102, 5], F32)
    d["TB"] = ("psum", [128, 6, 80], F32)
    return d


SCRATCH = bufs()
SEMAPHORES = ["od", "oh", "im", "imm", "hv", "hvl", "hm", "hml", "hl", "hll", "sto", "kc", "kg", "kh", "kp", "kq", "ks", "vo", "vh"] + ["e%d" % i for i in range(100)]


def rank_program(g, core, T, topo):
    rank = T.rank_of(core)
    if rank is None:
        return
    n = len(T.cores)
    prv, nxt = T.cores[(rank - 1) % n], T.cores[(rank + 1) % n]
    V, S, P, Y = g.vector, g.scalar, g.tensor, g.sync
    Q = {"v": V, "s": S, "p": P, "y": Y, "g": g}
    sem = T.sem
    total = {}
    seen = {}

    def ev(*calls):
        nm = "e%d" % len(total)
        total[nm] = len(calls)
        for c in calls:
            c.then_inc(sem[nm], 1)
        return nm

    def W(q, *evs):
        for e in evs:
            if (q, e) not in seen:
                seen[(q, e)] = 1
                Q[q].wait_ge(sem[e], total[e])

    def WD(q, s, v):
        if (q, s) not in seen:
            seen[(q, s)] = 1
            Q[q].wait_ge(sem[s], v)

    for b in (0, 1):
        Y.dma_start(out=T.WV[0:64, 2 * b:2 * b + 2, :], in_=T.vx[b::2, :]).then_inc(sem.od, 16)
        S.dma_start(out=T.WV[64:128, 2 * b:2 * b + 2, :], in_=T.vy[b::2, :]).then_inc(sem.od, 16)
    for b, a in ((4, 0), (5, 1536)):
        Y.dma_start(out=T.WV[0:64, b, :], in_=T.vx[:, a:a + 512]).then_inc(sem.oh, 16)
        S.dma_start(out=T.WV[64:128, b, :], in_=T.vy[:, a:a + 512]).then_inc(sem.oh, 16)
    Y.dma_start(out=T.IMG[:, 512:1024], in_=T.img[:, 0:512]).then_inc(sem.im, 16)
    S.dma_start(out=T.IMG[:, 2048:2560], in_=T.img[:, 1536:2048]).then_inc(sem.im, 16)
    Y.dma_start(out=T.IMG[:, 1024:2048], in_=T.img[:, 512:1536]).then_inc(sem.imm, 16)

    def iota(o, pat, b0, cm, sm):
        g.iota(o, pat, b0, cm, allow_small_or_imprecise_dtypes=True).then_inc(sm, 1)

    iota(T.K2[:], [[1, 2]], 0, 2, sem.kg)
    iota(T.K1[:], [[0, 2]], 0, 1, sem.kg)
    iota(T.RR[:, 0:2], [[0, 2]], 8, 0, sem.kg)
    iota(T.RR[:, 2:4], [[-40, 2]], 40, 0, sem.kg)
    iota(T.U[:], [[1, 144]], 0, 0, sem.kh)
    iota(T.kf[:], [[0, 1]], 0, 1, sem.ks)
    iota(T.V0[:, 2800:3200], [[0, 400]], 0, 0, sem.kp)
    kc = [0]

    def K(ins):
        ins.then_inc(sem.kc, 1)
        kc[0] += 1

    def KW():
        V.wait_ge(sem.kc, kc[0])

    ts, tt = V.tensor_scalar, V.tensor_tensor
    e0 = ev(V.memset(T.tc[0:64, :], -1.0))
    eZa = ev(V.memset(T.V0[:, 0:640], 0.0))
    K(V.memset(T.WB[:], 0.0))
    V.wait_ge(sem.kg, 4)
    K(ts(T.KR[:, 0:2], T.K2[:], 31, None, A.bitwise_and))
    K(ts(T.KR[:, 2:4], T.K1[:], 7, None, A.bitwise_and))
    exf = ev(ts(T.xf[:], T.K1[:, 0:1], 64.0, None, A.is_lt))
    KW()
    etc = ev(tt(T.tc[64:128, :], T.KR[64:128, :], T.RR[64:128, :], A.add))
    eZ = ev(V.memset(T.V0[:, 1200:2800], 0.0))
    W("s", eZa)
    eZb = ev(S.activation(T.V0[:, 640:1200], T.V0[:, 0:560], AF.Copy))
    S.wait_ge(sem.kh, 1)
    W("s", e0, exf, etc)
    etb = ev(*[S.activation(T.TB[:, s, 0:66], T.U[:, 0:66], AF.Identity, bias=T.tc[:, r:r + 1], scale=T.xf[:, 0:1])
               for s, r in enumerate((0, 1, 0, 1, 2, 3))])
    KW()
    V.wait_ge(sem.od, 64)
    V.wait_ge(sem.oh, 64)
    W("v", etb)
    eWB = ev(tt(T.WB[:, :, 8:72], T.WV[:], T.TB[:, :, 1:65], A.add),
             tt(T.WB[:, :, 7:73:65], T.WV[:, :, 0:64:63], T.TB[:, :, 0:66:65], A.add))
    for part, q in ((0, "y"), (1, "s")):
        W(q, eZ, eZb, eWB)
        Q[q].wait_ge(sem.kp, 1)
        for b in (0, 1):
            Q[q].dma_start(out=T.V0[16 * b + part::32, 640:3200], in_=T.WB[64 * part:64 * part + 64, 2 * b:2 * b + 2, :]).then_inc(sem.vo, 16)
    W("v", eWB)
    eWL = ev(V.tensor_copy(T.WL[:, :, :, 0:16], T.WB[:, 0:2, :]), S.activation(T.WL[:, :, :, 16:32], T.WB[:, 2:4, :], AF.Copy))
    eZh = ev(S.activation(T.V0[:, 3200:3840], T.V0[:, 0:640], AF.Copy))

    es = {d: topo.engines(core, d) for d in (prv, nxt)}
    h = min(len(es[prv]), len(es[nxt])) // 2

    def send(src_p, dst_p, src_n, dst_n, rs, ls):
        tr = []
        for d, s, o, lo in ((prv, src_p, dst_p, 0), (nxt, src_n, dst_n, h)):
            rid, pid, _ = topo.addr(d)
            tr.append(RemoteDMATransfer(dst_ids=[DstId(rid=rid, pnc=pid)], dma_engine_mask=sum(1 << e for e in es[d][lo:lo + h]),
                                        remote_sem=rs, src=s, dst=o))
        g.remote_dma_fused(tr, local_sem=ls)

    W("g", eWB)
    send(T.WB[:, 4, :], T.HL[:, 1, :], T.WB[:, 5, :], T.HL[:, 0, :], sem.hv, sem.hvl)
    iota(T.PI[:], [[9, 2], [1, 8]], -8, 0, sem.kq)

    W("y", eZa, eZh)
    Y.wait_ge(sem.hv, 2 * h)
    for side, a in ((0, 0), (1, 3200)):
        for part in (0, 1):
            Y.dma_start(out=T.V0[part::16, a:a + 640], in_=T.HL[64 * part:64 * part + 64, side, :]).then_inc(sem.vh, 16)

    V.wait_ge(sem.kh, 1)
    V.wait_ge(sem.ks, 1)
    eSD = ev(ts(T.SD[0:64, :], T.U[0:64, 0:64], T.kf[0:64, 0:1], 1.0, A.is_equal, A.mult),
             ts(T.SD[64:128, :], T.U[64:128, 64:128], T.kf[64:128, 0:1], 80.0, A.is_equal, A.mult))
    K(ts(T.b15[:], T.K1[:, 0:1], 15, None, A.bitwise_and))
    K(ts(T.m16[:], T.K1[:, 0:1], 112, None, A.bitwise_and))
    KW()
    K(ts(T.x0[:], T.b15[:], 0.0, None, A.is_equal))
    K(ts(T.t80[:], T.b15[:], 1.0, 80.0, A.is_equal, A.mult))
    K(ts(T.sc[:], T.m16[:], 15.0, None, A.add))
    KW()

    def pads(buf, i0, i1, w, *need):
        W("s", ePC, *need)
        W("v", ePC, *need)
        v, a, z = T[buf], 80 * (i0 + 8), 80 * (i1 + 8)
        c = []
        for k in range(1, w + 1):
            c.append(S.activation(v[:, a + 8 - k:z:80], v[:, a + 8:z:80], AF.Identity, bias=T.PC[:, 8 - k:9 - k]))
            c.append(ts(v[:, a + 71 + k:z:80], v[:, a + 71:z:80], T.PC[:, 7 + k:8 + k], None, A.add))
        return ev(*c)

    def wrap(sel, parts, *need):
        W("p", *need)
        last = []
        for out, src in parts:
            for q in range(16):
                ins = P.matmul(out, T[sel][:, 15 - q:143 - q], src(q), q == 0, q == 15)
            last.append(ins)
        return ev(*last)

    def vp(buf, i0, i1, s=0):
        return lambda q: T[buf][:, 80 * (i0 + 8) + s + q:80 * (i1 + 8) + s:16]

    def lst(out, src, i0, i1, *need):
        W("v", *need)
        return ev(ts(out, src, float(8 - 80 * (i0 + 8)), float(80 * (i1 - i0) - 1), A.add, A.min))

    def lst4(out, src, m, k, need):
        W("v", need)
        return ev(*[V.tensor_copy(out[:, b:4 * m:4], src[:, b:k * m:k] if b < k else src[:, k * m + b - k:4 * m:4 - k]) for b in range(4)])

    def gat(q, out, win, offs, need, clip=False):
        W(q, *need)
        if q == "s":
            return ev(S.activation(out, win.indirect(offs), AF.Relu if clip else AF.Copy))
        if clip:
            return ev(ts(out, win.indirect(offs), T.hi[:, 0:1], None, A.min))
        return ev(V.tensor_copy(out, win.indirect(offs)))

    def rows(buf, i0, i1):
        return T[buf][:, 80 * (i0 + 8):80 * (i1 + 8)]

    def blk(buf, i0, c0, c1):
        return T[buf][:, 80 * (i0 + 8) + 16 * c0:80 * (i0 + 8) + 16 * c1]

    W("p", eSD, eWL)
    w0 = ev(*[P.matmul(T.R0[32 * k:32 * k + 32, i:32:2, b], T.WL[:, i, b, :], T.SD[:, 16 * k:16 * k + 16], True, True)
              for b in range(5) for i in (0, 1) for k in range(4)])
    l0a = lst(T.L0I[:], T.R0[:, 1:31, :], 0, 32, w0)
    esl = ev(ts(T.SL[:, 0:30], T.R0[:, 0:6, :], 8.0 + 2560.0, 3839.0, A.add, A.min),
             ts(T.SL[:, 30:60], T.R0[:, 26:32, :], 8.0 - 2560.0, 3839.0, A.add, A.min))
    W("g", esl)
    send(T.SL[:, 0:30], T.LD[:], T.SL[:, 30:60], T.LT[:], sem.hl, sem.hll)
    g.wait_ge(sem.im, 32)
    send(T.IMG[:, 512:1024], T.IMG[:, 2560:3072], T.IMG[:, 2048:2560], T.IMG[:, 0:512], sem.hm, sem.hml)
    lx = ev(*[ts(T.LX[:, 6 * k:6 * k + 5], T.R0[:, 31 * k, :], 8.0, 3839.0, A.add, A.min) for k in (0, 1)])
    K(tt(T.w80[:], T.x0[:], T.t80[:], A.add))
    K(ts(T.t64[:], T.b15[:], 1.0, 64.0, A.is_equal, A.mult))

    for q in "vs":
        WD(q, "vo", 64)
    gas = gat("s", blk("V1", 1, 0, CA), rows("V0", 0, 32), T.L0I[:, 0:CA], [l0a])
    gav = gat("v", blk("V1", 1, CA, 80), rows("V0", 0, 32), T.L0I[:, CA:80], [l0a])
    KW()
    eS80 = ev(ts(T.S80[:], T.U[:], T.sc[:, 0:1], T.w80[:, 0:1], A.is_equal, A.mult))
    V.wait_ge(sem.kq, 1)
    ePC = ev(ts(T.PC[:], T.PI[:], T.x0[:, 0:1], None, A.mult))
    w1a = wrap("S80", [(T.P0[:, 0:NA], vp("V1", 3, G))], eS80, gas, gav)
    gbs = gat("s", blk("V1", 17, 0, CB), rows("V0", 0, 32), T.L0I[:, 80:80 + CB], [l0a])
    gbv = gat("v", blk("V1", 17, CB, 70), rows("V0", 0, 32), T.L0I[:, 80 + CB:150], [l0a])
    l1a = lst(T.L1I[:, 0:NA], T.P0[:, 0:NA], 1, G + 2, w1a)
    p1i = pads("V1", 1, 31, 2, gas, gav, gbs, gbv, w1a)
    in1 = [gas, gav, gbs, gbv, p1i]

    w1b = wrap("S80", [(T.P4[:, 0:NB], vp("V1", G, 29))], p1i)
    g1s = gat("s", blk("V2", 3, 0, C1), rows("V1", 1, G + 2), T.L1I[:, 0:C1], in1 + [l1a])
    g1v = gat("v", blk("V2", 3, C1, NA), rows("V1", 1, G + 2), T.L1I[:, C1:NA], in1 + [l1a])

    for q in "vs":
        WD(q, "vh", 64)
        WD(q, "hl", 2 * h)
    h0s = gat("s", rows("V1", -6, 0), T.V0[:], T.LT[:], [])
    h0v = gat("v", rows("V1", 32, 38), T.V0[:], T.LD[:], [])
    h0w = gat("s", rows("V1", 0, 1), T.V0[:], T.LX[:, 0:5], [lx])
    h0x = gat("v", rows("V1", 31, 32), T.V0[:], T.LX[:, 6:11], [lx])
    l1b = lst(T.L1I[:, 70:70 + NB], T.P4[:, 0:NB], G - 2, 31, w1b)
    p1h = pads("V1", -6, 38, 2, h0s, h0v, h0w, h0x, w1b, g1s, g1v)
    all1 = in1 + [h0s, h0v, h0w, h0x, p1h]
    w1h = wrap("S80", [(T.P0[:, 0:40], vp("V1", -4, 4)), (T.P0[:, 40:75], vp("V1", 29, 36))], l1a, *all1)

    g2s = gat("s", blk("V2", G, 0, C2), rows("V1", G - 2, 31), T.L1I[:, 70:70 + C2], all1 + [l1b])
    g2v = gat("v", blk("V2", G, C2, NB), rows("V1", G - 2, 31), T.L1I[:, 70 + C2:70 + NB], all1 + [l1b])
    w2i = wrap("S80", [(T.R1[:, 0:M, :], vp("V2", IO, IO + M, 8))], g1s, g1v, g2s, g2v)
    K(tt(T.w64[:], T.x0[:], T.t64[:], A.add))
    K(ts(T.hi[:], T.x0[:], 63.0 - 1024.0, 1024.0, A.mult, A.add))
    KW()
    l1h = lst(T.L1H[:, 0:75], T.P0[:, 0:75], -6, 38, w1h)
    h1s = gat("s", rows("V2", -4, 3), rows("V1", -6, 38), T.L1H[:, 0:35], all1 + [l1h])
    h1v = gat("v", blk("V2", 29, 0, D1), rows("V1", -6, 38), T.L1H[:, 40:40 + D1], all1 + [l1h])
    h1w = gat("s", blk("V2", 29, D1, 35), rows("V1", -6, 38), T.L1H[:, 40 + D1:75], all1 + [l1h])
    p2 = pads("V2", -4, 36, 4, h1s, h1v, h1w, g1s, g1v, g2s, g2v, w2i)
    all2 = [h1s, h1v, h1w, g1s, g1v, g2s, g2v, p2]
    w2h = wrap("S80", [(T.R0[:, 0:IO, :], vp("V2", 0, IO, 8)), (T.R0[:, IO:2 * IO, :], vp("V2", 32 - IO, 32, 8))], l0a, esl, lx, *all2)

    l2l = lst(T.L2IL[:], T.R1[:, 0:M, 0:2], IO - 4, IO + M + 4, w2i)
    l2r = lst(T.L2IR[:], T.R1[:, 0:M, 2:4], IO - 4, IO + M + 4)
    i2s = gat("s", T.PHI[:, 0:32 * M], rows("V2", IO - 4, IO + M + 4), T.L2IL[:], all2 + [l2l], True)
    i2v = gat("v", T.PHI[:, 32 * M:64 * M], rows("V2", IO - 4, IO + M + 4), T.L2IR[:], all2 + [l2r], True)
    eS64 = ev(ts(T.S64[:], T.U[:], T.sc[:, 0:1], T.w64[:, 0:1], A.is_equal, A.mult))
    w3i = wrap("S64", [(T.P1[:, 0:4 * M], lambda q: T.PHI[:, q:64 * M:16])], eS64, i2s, i2v)
    l2hl = lst(T.L2HL[:, 0:2 * IO * KL], T.R0[:, 0:2 * IO, 0:KL], -4, 36, w2h)
    l2hr = lst(T.L2HR[:, 0:2 * IO * (4 - KL)], T.R0[:, 0:2 * IO, KL:4], -4, 36)
    h2s = gat("s", T.PHH[:, 0:32 * IO * KL], rows("V2", -4, 36), T.L2HL[:, 0:2 * IO * KL], all2 + [l2hl], True)
    h2v = gat("v", T.PHH[:, 32 * IO * KL:128 * IO], rows("V2", -4, 36), T.L2HR[:, 0:2 * IO * (4 - KL)], all2 + [l2hr], True)
    w3h = wrap("S64", [(T.P2[:, 0:8 * IO], lambda q: T.PHH[:, q:128 * IO:16])], h2s, h2v)

    l3i = lst4(T.L3I, T.P1, M, 2, w3i)
    for q in (V, S):
        q.wait_ge(sem.im, 32)
        q.wait_ge(sem.imm, 16)
        q.wait_ge(sem.hm, 2 * h)
    yi, ym, yj = IO * 64, (IO + A3) * 64, (IO + M) * 64
    g3s = gat("s", T.Y[:, yi:ym], T.IMG[:], T.L3I[:, 0:4 * A3], [l3i])
    g3v = gat("v", T.Y[:, ym:yj], T.IMG[:], T.L3I[:, 4 * A3:4 * M], [l3i])
    W("y", g3s, g3v)
    Y.dma_start(out=T.y[:, yi:yj], in_=T.Y[:, yi:yj]).then_inc(sem.sto, 16)

    l3h = lst4(T.L3H, T.P2, 2 * IO, KL, w3h)
    h3s = gat("s", T.Y[:, 0:yi], T.IMG[:], T.L3H[:, 0:4 * IO], [l3h])
    h3v = gat("v", T.Y[:, yj:2048], T.IMG[:], T.L3H[:, 4 * IO:8 * IO], [l3h])
    W("s", h3s)
    S.dma_start(out=T.y[:, 0:yi], in_=T.Y[:, 0:yi]).then_inc(sem.sto, 16)
    W("y", h3v)
    Y.dma_start(out=T.y[:, yj:2048], in_=T.Y[:, yj:2048]).then_inc(sem.sto, 16)

    Y.wait_ge(sem.sto, 48)
    g.wait_ge(sem.hvl, 2 * h)
    g.wait_ge(sem.hml, 2 * h)
    g.wait_ge(sem.hll, 2 * h)
